import numpy as np
import ml_dtypes


def mxq(x, axis, fmt="e4m3"):
    dtype, down = {"e4m3": (ml_dtypes.float8_e4m3fn, 7), "e5m2": (ml_dtypes.float8_e5m2, 14)}[fmt]
    v = np.moveaxis(np.asarray(x, np.float32).astype(ml_dtypes.bfloat16).astype(np.float64), axis, -1)
    blocks = v.reshape(v.shape[:-1] + (-1, 32))
    amax = np.abs(blocks).max(-1, keepdims=True)
    byte = np.maximum(np.where(amax > 0, np.frexp(amax)[1] - 1 + 127, 0) - down, 1)
    scale = np.exp2(byte - 127.0)
    codes = (blocks / scale).astype(np.float32).astype(dtype).astype(np.float64)
    return np.moveaxis((codes * scale).reshape(v.shape), -1, axis)


WIDE = False


def mx_kscale(k, group=512):
    if not WIDE:
        return np.ones(k)
    levels = np.array([10, -10, 5, -5, 0])
    if group != 512:
        return np.exp2(np.random.permutation(np.resize(levels, k // group))).repeat(group)
    if k % 512:
        return np.exp2(np.random.permutation(np.resize(levels, k // 32))).repeat(32)
    a = np.empty((k // 512, 16))
    for p in range(k // 512):
        a[p, :8] = np.random.permutation(np.resize(levels, 8))
        for g in range(8):
            far = levels[np.abs(levels - a[p, g]) >= 10]
            a[p, g + 8] = far[np.random.randint(len(far))]
    return np.exp2(a.ravel()).repeat(32)


def f64(x):
    return np.asarray(x).astype(np.float64)


def striped(idx):
    return np.tile(np.asarray(idx).reshape(-1, 16).T, (8, 1)).astype(np.uint16)


def unstriped(offs):
    return offs[:16].T.reshape(-1).astype(np.int64)


H, KV, D, NQ, N = 4, 2, 256, 512, 512


def setup_inputs():
    n = np.random.standard_normal
    s = mx_kscale(D, 0)[:, None]
    u = mx_kscale(N)
    t = np.random.uniform(0.5, 2.0, N) * u
    v = n((KV, N, 128))
    return {
        "qT": (n((H, D, NQ)) * s * (0.70 / np.sqrt(D))).astype(np.float32),
        "kT": (n((KV, D, N)) / s).astype(np.float32),
        "t": t.reshape(N, 1).astype(np.float32),
        "v": (v / t[:, None]).astype(np.float32),
        "mask": (np.arange(N)[:, None] <= np.sort(np.random.randint(N // 4, N, NQ))[None, :]).astype(np.float32),
        "og": n((H, NQ, 128)).astype(np.float32),
    }


def reference(qT, kT, t, v, mask, og):
    a = np.repeat(mxq(f64(kT), 1, "e4m3"), H // KV, 0).transpose(0, 2, 1) @ mxq(f64(qT), 1, "e4m3")
    p = np.maximum(a, 0.0)
    p = p * f64(mask)
    w = p * f64(t)
    y = mxq(w, 1, "e4m3").transpose(0, 2, 1) @ np.repeat(mxq(f64(v), 1, "e4m3"), H // KV, 0)
    y = y / 16.0
    y = y / (1.0 + np.exp(-f64(og)))
    return y

@@ -1,0 +1,261 @@
+from contextlib import ExitStack
+
+import concourse.mybir as mybir
+
+H, KV, D, NQ, N, E = 4, 2, 256, 512, 512, 128
+FLOPS = 2 * H * N * NQ * D + 2 * H * NQ * N * E
+
+F32 = mybir.dt.float32
+BF16 = mybir.dt.bfloat16
+I32 = mybir.dt.int32
+U8 = mybir.dt.uint8
+FP8X4 = mybir.dt.float8_e4m3fn_x4
+ALU = mybir.AluOpType
+ACT = mybir.ActivationFunctionType
+
+P = 128
+ROWS = 64
+PACK = 4
+QC = 128
+CHUNKS = NQ // QC
+K_SPLIT = 84
+SCORE_BANKS = 3
+MT_ON_VECTOR = (0, 1)
+
+
+def tile_rows_a_relu_mask_gate_kernel(tc, qT, kT, t, v, mask, og, out):
+    nc = tc.nc
+    with ExitStack() as ctx:
+        sb = ctx.enter_context(tc.tile_pool(name="sb", bufs=1))
+        ps = ctx.enter_context(tc.psum_pool(name="ps", bufs=1))
+        ctx.enter_context(tc.manual_schedule())
+
+        def tile(name, shape, dtype):
+            return sb.tile(shape, dtype, name=name, align_bytes=64)
+
+        t_sb = tile("t_sb", [P, PACK], F32)
+        warm = tile("warm", [P, 2], F32)
+        k_raw = tile("k_raw", [P, PACK, N], F32)
+        k_bf = tile("k_bf", [P, PACK, P, PACK], BF16)
+        k_mx = tile("k_mx", [P, N + N // 4], I32)
+        k_swap = tile("k_swap", [P, N + N // 4], I32)
+        v_raw = tile("v_raw", [P, KV, PACK, E], F32)
+        v_bf = tile("v_bf", [P, KV, E, PACK], BF16)
+        v_codes = tile("v_codes", [P, KV * E], I32)
+        v_scales = tile("v_scales", [P, KV * E], U8)
+        pairs = [(a, c) for c in range(CHUNKS) for a in range(2)]
+        q_raw = {x: tile("q_raw%d%d" % x, [P, PACK, QC], F32) for x in pairs}
+        q_bf = {x: tile("q_bf%d%d" % x, [P, QC, PACK], BF16) for x in pairs}
+        q_codes = {x: tile("q_codes%d%d" % x, [P, QC], I32) for x in pairs}
+        q_scales = {x: tile("q_scales%d%d" % x, [P, QC], U8) for x in pairs}
+        w_bf = {x: tile("w_bf%d%d" % x, [P, 2, QC, PACK], BF16) for x in pairs}
+        w_codes = {x: tile("w_codes%d%d" % x, [P, 2 * QC], I32) for x in pairs}
+        w_scales = {x: tile("w_scales%d%d" % x, [P, 2 * QC], U8) for x in pairs}
+        m_raw = [tile("m_raw%d" % c, [P, PACK, QC], F32) for c in range(CHUNKS)]
+        m_scaled = [tile("m_scaled%d" % c, [P, PACK, QC], F32) for c in range(CHUNKS)]
+        mt = [tile("mt%d" % c, [P, QC, PACK], F32) for c in range(CHUNKS)]
+        og_raw = [tile("og_raw%d" % c, [P, H, E], F32) for c in range(CHUNKS)]
+        gate = [tile("gate%d" % c, [P, H, E], F32) for c in range(CHUNKS)]
+        res = [tile("res%d" % c, [P, H, E], F32) for c in range(CHUNKS)]
+        score_banks = [
+            [ps.tile([P, PACK, QC], F32, name="score%d%d" % (g, b)) for b in range(SCORE_BANKS)] for g in range(2)
+        ]
+        y_banks = [ps.tile([P, H, E], F32, name="y%d" % b) for b in range(2)]
+
+        def cols(c):
+            return slice(c * QC, (c + 1) * QC)
+
+        def load_q(a, c):
+            rows = qT[2 * a : 2 * a + 2].rearrange("g (p j) q -> (g p) j q", j=PACK)
+            nc.sync.dma_start(out=q_raw[a, c][:], in_=rows[:, :, cols(c)])
+
+        def load_mask(c):
+            nc.sync.dma_start(out=m_raw[c][:], in_=mask.rearrange("(s r) q -> s r q", r=PACK)[:, :, cols(c)])
+
+        def load_og(c):
+            nc.sync.dma_start(out=og_raw[c][:], in_=og[:, cols(c), :].rearrange("h q e -> q h e"))
+
+        def cast_q(a, c):
+            nc.scalar.copy(
+                out=q_bf[a, c][:].rearrange("p (c i) j -> p c j i", i=4),
+                in_=q_raw[a, c][:].rearrange("p j (c i) -> p c j i", i=4),
+            )
+
+        def quant_q(a, c):
+            nc.vector.quantize_mx(
+                out=q_codes[a, c][:].bitcast(FP8X4),
+                scales=q_scales[a, c][:],
+                in_=q_bf[a, c][:].rearrange("p q j -> p (q j)"),
+            )
+
+        def make_mt(c):
+            if c in MT_ON_VECTOR:
+                nc.vector.tensor_tensor(
+                    out=mt[c][:],
+                    in0=m_raw[c][:].rearrange("p r q -> p q r"),
+                    in1=t_sb[:, 0:PACK].unsqueeze(1).to_broadcast([P, QC, PACK]),
+                    op=ALU.mult,
+                )
+            else:
+                for r in range(PACK):
+                    nc.scalar.activation(
+                        out=m_scaled[c][:, r, :], in_=m_raw[c][:, r, :], func=ACT.Copy, scale=t_sb[:, r : r + 1]
+                    )
+                nc.scalar.copy(out=mt[c][:], in_=m_scaled[c][:].rearrange("p r q -> p q r"))
+
+        def bank(h, c):
+            return score_banks[h % 2][(2 * c + h // 2) % SCORE_BANKS]
+
+        def scores(heads, c):
+            for r in range(PACK):
+                for h in heads:
+                    g = h % 2
+                    rows = slice(ROWS * g, ROWS * (g + 1))
+                    keys = k_mx if h // 2 == g else k_swap
+                    nc.tensor.matmul_mx(
+                        out=bank(h, c)[:, r, :],
+                        lhsT=keys[rows, r * P : (r + 1) * P].bitcast(FP8X4),
+                        lhsT_scale=keys[rows, N:].bitcast(U8)[:, r * P : (r + 1) * P],
+                        rhs=q_codes[h // 2, c][rows, :].bitcast(FP8X4),
+                        rhs_scale=q_scales[h // 2, c][rows, :],
+                        start=True,
+                        stop=True,
+                    )
+
+        def weigh(h, c):
+            nc.vector.scalar_tensor_tensor(
+                out=w_bf[h // 2, c][:, h % 2],
+                in0=bank(h, c)[:].rearrange("p r q -> p q r"),
+                scalar=0.0,
+                in1=mt[c][:],
+                op0=ALU.max,
+                op1=ALU.mult,
+            )
+
+        def quant_w(a, c):
+            nc.vector.quantize_mx(
+                out=w_codes[a, c][:].bitcast(FP8X4),
+                scales=w_scales[a, c][:],
+                in_=w_bf[a, c][:].rearrange("p g q r -> p (g q r)"),
+            )
+
+        def values(a, c):
+            for g in range(2):
+                nc.tensor.matmul_mx(
+                    out=y_banks[c % 2][:, 2 * a + g, :],
+                    lhsT=w_codes[a, c][:, g * QC : (g + 1) * QC].bitcast(FP8X4),
+                    lhsT_scale=w_scales[a, c][:, g * QC : (g + 1) * QC],
+                    rhs=v_codes[:, a * E : (a + 1) * E].bitcast(FP8X4),
+                    rhs_scale=v_scales[:, a * E : (a + 1) * E],
+                    start=True,
+                    stop=True,
+                )
+
+        def sigmoid(c):
+            nc.scalar.activation(out=gate[c][:], in_=og_raw[c][:], func=ACT.Sigmoid)
+
+        def finish(c, heads):
+            nc.vector.scalar_tensor_tensor(
+                out=res[c][:, heads],
+                in0=y_banks[c % 2][:, heads],
+                scalar=1.0 / 16.0,
+                in1=gate[c][:, heads],
+                op0=ALU.mult,
+                op1=ALU.mult,
+            )
+            nc.sync.dma_start(out=out[heads, cols(c), :].rearrange("h q e -> q h e"), in_=res[c][:, heads])
+
+        nc.sync.dma_start(out=k_raw[:], in_=kT.rearrange("g (p j) n -> (g p) j n", j=PACK))
+        load_q(0, 0)
+        load_mask(0)
+        load_q(1, 0)
+        nc.scalar.dma_start(out=t_sb[:], in_=t.rearrange("(s r) o -> s (r o)", r=PACK))
+        nc.vector.memset(warm[:, 0:1], 0.0)
+        nc.vector.memset(k_mx[:, N:], 0)
+        nc.scalar.activation(out=warm[:, 1:2], in_=warm[:, 0:1], func=ACT.Sigmoid)
+
+        k_src = k_raw[:].rearrange("p j (s r) -> p s r j", r=PACK)
+        k_dst = k_bf[:].rearrange("p r s j -> p s r j")
+        nc.vector.tensor_copy(out=k_dst[:, :K_SPLIT], in_=k_src[:, :K_SPLIT])
+        nc.scalar.copy(out=k_dst[:, K_SPLIT:], in_=k_src[:, K_SPLIT:])
+        cast_q(0, 0)
+        nc.vector.quantize_mx(
+            out=k_mx[:, :N].bitcast(FP8X4),
+            scales=k_mx[:, N:].bitcast(U8),
+            in_=k_bf[:].rearrange("p r s j -> p (r s j)"),
+        )
+        nc.scalar.dma_start(out=k_swap[ROWS:, :], in_=k_mx[:ROWS, :])
+        nc.scalar.dma_start(out=k_swap[:ROWS, :], in_=k_mx[ROWS:, :])
+
+        load_q(0, 1)
+        load_mask(1)
+        load_q(1, 1)
+        nc.sync.dma_start(
+            out=v_raw[:].rearrange("p g j e -> p g (j e)"), in_=v.rearrange("g (p j) e -> p g (j e)", j=PACK)
+        )
+        for c in range(2, CHUNKS):
+            load_q(0, c)
+            load_mask(c)
+            load_q(1, c)
+            load_og(c - 2)
+        load_og(CHUNKS - 2)
+        load_og(CHUNKS - 1)
+
+        quant_q(0, 0)
+        scores([0], 0)
+        make_mt(0)
+        cast_q(1, 0)
+        weigh(0, 0)
+        quant_q(1, 0)
+        scores([3], 0)
+        scores([1], 0)
+        scores([2], 0)
+        cast_q(0, 1)
+        make_mt(1)
+        weigh(3, 0)
+        cast_q(1, 1)
+        weigh(1, 0)
+        quant_q(0, 1)
+        scores([0, 1], 1)
+        weigh(2, 0)
+        quant_w(0, 0)
+        quant_q(1, 1)
+        scores([2, 3], 1)
+        nc.scalar.copy(
+            out=v_bf[:].rearrange("p g (c i) j -> p g c j i", i=4),
+            in_=v_raw[:].rearrange("p g j (c i) -> p g c j i", i=4),
+        )
+
+        for c in range(1, CHUNKS):
+            last = c == CHUNKS - 1
+            if not last:
+                cast_q(0, c + 1)
+                make_mt(c + 1)
+                cast_q(1, c + 1)
+            sigmoid(c - 1)
+            if last:
+                sigmoid(c)
+            weigh(0, c)
+            quant_w(1, c - 1)
+            weigh(1, c)
+            if c == 1:
+                nc.vector.quantize_mx(
+                    out=v_codes[:].bitcast(FP8X4), scales=v_scales[:], in_=v_bf[:].rearrange("p g e j -> p (g e j)")
+                )
+                values(0, 0)
+            values(1, c - 1)
+            if not last:
+                quant_q(0, c + 1)
+                scores([0, 1], c + 1)
+            weigh(2, c)
+            quant_w(0, c)
+            finish(c - 1, slice(0, H))
+            values(0, c)
+            weigh(3, c)
+            if not last:
+                quant_q(1, c + 1)
+                scores([2, 3], c + 1)
+        finish(CHUNKS - 1, slice(0, 2))
+        quant_w(1, CHUNKS - 1)
+        values(1, CHUNKS - 1)
+        finish(CHUNKS - 1, slice(2, H))

@@ -20,7 +20,6 @@ QC = 128
 CHUNKS = NQ // QC
 K_SPLIT = 84
 SCORE_BANKS = 3
-MT_ON_VECTOR = (0, 1)
 
 
 def tile_rows_a_relu_mask_gate_kernel(tc, qT, kT, t, v, mask, og, out):
@@ -38,47 +37,53 @@ def tile_rows_a_relu_mask_gate_kernel(tc, qT, kT, t, v, mask, og, out):
         k_raw = tile("k_raw", [P, PACK, N], F32)
         k_bf = tile("k_bf", [P, PACK, P, PACK], BF16)
         k_mx = tile("k_mx", [P, N + N // 4], I32)
-        k_swap = tile("k_swap", [P, N + N // 4], I32)
+        k_up = tile("k_up", [P, N + N // 4], I32)
+        k_down = tile("k_down", [P, N + N // 4], I32)
         v_raw = tile("v_raw", [P, KV, PACK, E], F32)
         v_bf = tile("v_bf", [P, KV, E, PACK], BF16)
         v_codes = tile("v_codes", [P, KV * E], I32)
         v_scales = tile("v_scales", [P, KV * E], U8)
         pairs = [(a, c) for c in range(CHUNKS) for a in range(2)]
-        q_raw = {x: tile("q_raw%d%d" % x, [P, PACK, QC], F32) for x in pairs}
+        q_half = {(a, u): tile("q_half%d%d" % (a, u), [P, PACK, 2 * QC], F32) for a in range(2) for u in range(2)}
         q_bf = {x: tile("q_bf%d%d" % x, [P, QC, PACK], BF16) for x in pairs}
         q_codes = {x: tile("q_codes%d%d" % x, [P, QC], I32) for x in pairs}
         q_scales = {x: tile("q_scales%d%d" % x, [P, QC], U8) for x in pairs}
-        w_bf = {x: tile("w_bf%d%d" % x, [P, 2, QC, PACK], BF16) for x in pairs}
-        w_codes = {x: tile("w_codes%d%d" % x, [P, 2 * QC], I32) for x in pairs}
-        w_scales = {x: tile("w_scales%d%d" % x, [P, 2 * QC], U8) for x in pairs}
-        m_raw = [tile("m_raw%d" % c, [P, PACK, QC], F32) for c in range(CHUNKS)]
-        m_scaled = [tile("m_scaled%d" % c, [P, PACK, QC], F32) for c in range(CHUNKS)]
+        halves = [(h, u) for h in range(H) for u in range(2)]
+        w_bf = {x: tile("w_bf%d%d" % x, [P, 2, QC, PACK], BF16) for x in halves}
+        w_codes = {x: tile("w_codes%d%d" % x, [P, 2 * QC], I32) for x in halves}
+        w_scales = {x: tile("w_scales%d%d" % x, [P, 2 * QC], U8) for x in halves}
+        m_half = [tile("m_half%d" % u, [P, PACK, 2 * QC], F32) for u in range(2)]
+        m_scaled = tile("m_scaled", [P, PACK, 2 * QC], F32)
         mt = [tile("mt%d" % c, [P, QC, PACK], F32) for c in range(CHUNKS)]
-        og_raw = [tile("og_raw%d" % c, [P, H, E], F32) for c in range(CHUNKS)]
-        gate = [tile("gate%d" % c, [P, H, E], F32) for c in range(CHUNKS)]
-        res = [tile("res%d" % c, [P, H, E], F32) for c in range(CHUNKS)]
+        og_raw = [tile("og_raw%d" % h, [P, CHUNKS, E], F32) for h in range(H)]
+        gate = [tile("gate%d" % h, [P, CHUNKS, E], F32) for h in range(H)]
+        res = [tile("res%d" % h, [P, CHUNKS, E], F32) for h in range(H)]
         score_banks = [
             [ps.tile([P, PACK, QC], F32, name="score%d%d" % (g, b)) for b in range(SCORE_BANKS)] for g in range(2)
         ]
-        y_banks = [ps.tile([P, H, E], F32, name="y%d" % b) for b in range(2)]
+        y_banks = [ps.tile([P, CHUNKS, E], F32, name="y%d" % b) for b in range(2)]
 
         def cols(c):
             return slice(c * QC, (c + 1) * QC)
 
-        def load_q(a, c):
-            rows = qT[2 * a : 2 * a + 2].rearrange("g (p j) q -> (g p) j q", j=PACK)
-            nc.sync.dma_start(out=q_raw[a, c][:], in_=rows[:, :, cols(c)])
+        def q_rows(a):
+            return qT[2 * a : 2 * a + 2].rearrange("g (p j) q -> (g p) j q", j=PACK)
 
-        def load_mask(c):
-            nc.sync.dma_start(out=m_raw[c][:], in_=mask.rearrange("(s r) q -> s r q", r=PACK)[:, :, cols(c)])
+        def load_q(a, u):
+            nc.sync.dma_start(out=q_half[a, u][:], in_=q_rows(a)[:, :, 2 * u * QC : 2 * (u + 1) * QC])
 
-        def load_og(c):
-            nc.sync.dma_start(out=og_raw[c][:], in_=og[:, cols(c), :].rearrange("h q e -> q h e"))
+        def load_mask(u):
+            rows = mask.rearrange("(s r) q -> s r q", r=PACK)
+            nc.sync.dma_start(out=m_half[u][:], in_=rows[:, :, 2 * u * QC : 2 * (u + 1) * QC])
+
+        def load_og(h):
+            nc.sync.dma_start(out=og_raw[h][:], in_=og[h].rearrange("(c q) e -> q c e", q=QC))
 
         def cast_q(a, c):
+            raw = q_half[a, c // 2][:, :, cols(c % 2)]
             nc.scalar.copy(
                 out=q_bf[a, c][:].rearrange("p (c i) j -> p c j i", i=4),
-                in_=q_raw[a, c][:].rearrange("p j (c i) -> p c j i", i=4),
+                in_=raw.rearrange("p j (c i) -> p c j i", i=4),
             )
 
         def quant_q(a, c):
@@ -88,43 +93,47 @@ def tile_rows_a_relu_mask_gate_kernel(tc, qT, kT, t, v, mask, og, out):
                 in_=q_bf[a, c][:].rearrange("p q j -> p (q j)"),
             )
 
-        def make_mt(c):
-            if c in MT_ON_VECTOR:
-                nc.vector.tensor_tensor(
-                    out=mt[c][:],
-                    in0=m_raw[c][:].rearrange("p r q -> p q r"),
-                    in1=t_sb[:, 0:PACK].unsqueeze(1).to_broadcast([P, QC, PACK]),
-                    op=ALU.mult,
+        def mt_vector(c):
+            nc.vector.tensor_tensor(
+                out=mt[c][:],
+                in0=m_half[c // 2][:, :, cols(c % 2)].rearrange("p r q -> p q r"),
+                in1=t_sb[:, 0:PACK].unsqueeze(1).to_broadcast([P, QC, PACK]),
+                op=ALU.mult,
+            )
+
+        def scale_mask(u):
+            for r in range(PACK):
+                nc.scalar.activation(
+                    out=m_scaled[:, r, :], in_=m_half[u][:, r, :], func=ACT.Copy, scale=t_sb[:, r : r + 1]
                 )
-            else:
-                for r in range(PACK):
-                    nc.scalar.activation(
-                        out=m_scaled[c][:, r, :], in_=m_raw[c][:, r, :], func=ACT.Copy, scale=t_sb[:, r : r + 1]
-                    )
-                nc.scalar.copy(out=mt[c][:], in_=m_scaled[c][:].rearrange("p r q -> p q r"))
+
+        def mt_scalar(c):
+            nc.scalar.copy(out=mt[c][:], in_=m_scaled[:, :, cols(c % 2)].rearrange("p r q -> p q r"))
+
+        bank_of = {}
 
         def bank(h, c):
-            return score_banks[h % 2][(2 * c + h // 2) % SCORE_BANKS]
+            return bank_of[h, c]
 
-        def scores(heads, c):
+        def scores(h, c):
+            g = h % 2
+            bank_of[h, c] = score_banks[g][sum(1 for x in bank_of if x[0] % 2 == g) % SCORE_BANKS]
+            rows = slice(ROWS * g, ROWS * (g + 1))
+            keys = (k_mx, k_up, k_down, k_mx)[h]
             for r in range(PACK):
-                for h in heads:
-                    g = h % 2
-                    rows = slice(ROWS * g, ROWS * (g + 1))
-                    keys = k_mx if h // 2 == g else k_swap
-                    nc.tensor.matmul_mx(
-                        out=bank(h, c)[:, r, :],
-                        lhsT=keys[rows, r * P : (r + 1) * P].bitcast(FP8X4),
-                        lhsT_scale=keys[rows, N:].bitcast(U8)[:, r * P : (r + 1) * P],
-                        rhs=q_codes[h // 2, c][rows, :].bitcast(FP8X4),
-                        rhs_scale=q_scales[h // 2, c][rows, :],
-                        start=True,
-                        stop=True,
-                    )
+                nc.tensor.matmul_mx(
+                    out=bank(h, c)[:, r, :],
+                    lhsT=keys[rows, r * P : (r + 1) * P].bitcast(FP8X4),
+                    lhsT_scale=keys[rows, N:].bitcast(U8)[:, r * P : (r + 1) * P],
+                    rhs=q_codes[h // 2, c][rows, :].bitcast(FP8X4),
+                    rhs_scale=q_scales[h // 2, c][rows, :],
+                    start=True,
+                    stop=True,
+                )
 
         def weigh(h, c):
             nc.vector.scalar_tensor_tensor(
-                out=w_bf[h // 2, c][:, h % 2],
+                out=w_bf[h, c // 2][:, c % 2],
                 in0=bank(h, c)[:].rearrange("p r q -> p q r"),
                 scalar=0.0,
                 in1=mt[c][:],
@@ -132,44 +141,56 @@ def tile_rows_a_relu_mask_gate_kernel(tc, qT, kT, t, v, mask, og, out):
                 op1=ALU.mult,
             )
 
-        def quant_w(a, c):
+        def quant_w(h, c0, c1):
+            u, x = divmod(c0, 2)
+            span = slice(x * QC, (x + c1 - c0) * QC)
             nc.vector.quantize_mx(
-                out=w_codes[a, c][:].bitcast(FP8X4),
-                scales=w_scales[a, c][:],
-                in_=w_bf[a, c][:].rearrange("p g q r -> p (g q r)"),
+                out=w_codes[h, u][:, span].bitcast(FP8X4),
+                scales=w_scales[h, u][:, span],
+                in_=w_bf[h, u][:, x : x + c1 - c0].rearrange("p c q r -> p (c q r)"),
             )
 
-        def values(a, c):
-            for g in range(2):
+        def y_slot(h, c0, c1):
+            b = h % 2
+            return y_banks[b][:, c0:c1]
+
+        def values(h, c0, c1):
+            for c in range(c0, c1):
+                u, x = divmod(c, 2)
                 nc.tensor.matmul_mx(
-                    out=y_banks[c % 2][:, 2 * a + g, :],
-                    lhsT=w_codes[a, c][:, g * QC : (g + 1) * QC].bitcast(FP8X4),
-                    lhsT_scale=w_scales[a, c][:, g * QC : (g + 1) * QC],
-                    rhs=v_codes[:, a * E : (a + 1) * E].bitcast(FP8X4),
-                    rhs_scale=v_scales[:, a * E : (a + 1) * E],
+                    out=y_slot(h, c, c + 1)[:, 0, :],
+                    lhsT=w_codes[h, u][:, x * QC : (x + 1) * QC].bitcast(FP8X4),
+                    lhsT_scale=w_scales[h, u][:, x * QC : (x + 1) * QC],
+                    rhs=v_codes[:, (h // 2) * E : (h // 2 + 1) * E].bitcast(FP8X4),
+                    rhs_scale=v_scales[:, (h // 2) * E : (h // 2 + 1) * E],
                     start=True,
                     stop=True,
                 )
 
-        def sigmoid(c):
-            nc.scalar.activation(out=gate[c][:], in_=og_raw[c][:], func=ACT.Sigmoid)
+        def sigmoid(h):
+            nc.scalar.activation(out=gate[h][:], in_=og_raw[h][:], func=ACT.Sigmoid)
 
-        def finish(c, heads):
+        def store(h, c0, c1):
+            nc.sync.dma_start(out=out[h].rearrange("(c q) e -> q c e", q=QC)[:, c0:c1], in_=res[h][:, c0:c1])
+
+        def finish(h, c0, c1):
             nc.vector.scalar_tensor_tensor(
-                out=res[c][:, heads],
-                in0=y_banks[c % 2][:, heads],
+                out=res[h][:, c0:c1],
+                in0=y_slot(h, c0, c1),
                 scalar=1.0 / 16.0,
-                in1=gate[c][:, heads],
+                in1=gate[h][:, c0:c1],
                 op0=ALU.mult,
                 op1=ALU.mult,
             )
-            nc.sync.dma_start(out=out[heads, cols(c), :].rearrange("h q e -> q h e"), in_=res[c][:, heads])
+            store(h, c0, c1)
 
         nc.sync.dma_start(out=k_raw[:], in_=kT.rearrange("g (p j) n -> (g p) j n", j=PACK))
+        nc.scalar.dma_start(out=t_sb[:], in_=t.rearrange("(s r) o -> s (r o)", r=PACK))
         load_q(0, 0)
         load_mask(0)
         load_q(1, 0)
-        nc.scalar.dma_start(out=t_sb[:], in_=t.rearrange("(s r) o -> s (r o)", r=PACK))
+        load_q(0, 1)
+        load_mask(1)
         nc.vector.memset(warm[:, 0:1], 0.0)
         nc.vector.memset(k_mx[:, N:], 0)
         nc.scalar.activation(out=warm[:, 1:2], in_=warm[:, 0:1], func=ACT.Sigmoid)
@@ -178,84 +199,108 @@ def tile_rows_a_relu_mask_gate_kernel(tc, qT, kT, t, v, mask, og, out):
         k_dst = k_bf[:].rearrange("p r s j -> p s r j")
         nc.vector.tensor_copy(out=k_dst[:, :K_SPLIT], in_=k_src[:, :K_SPLIT])
         nc.scalar.copy(out=k_dst[:, K_SPLIT:], in_=k_src[:, K_SPLIT:])
-        cast_q(0, 0)
         nc.vector.quantize_mx(
             out=k_mx[:, :N].bitcast(FP8X4),
             scales=k_mx[:, N:].bitcast(U8),
             in_=k_bf[:].rearrange("p r s j -> p (r s j)"),
         )
-        nc.scalar.dma_start(out=k_swap[ROWS:, :], in_=k_mx[:ROWS, :])
-        nc.scalar.dma_start(out=k_swap[:ROWS, :], in_=k_mx[ROWS:, :])
-
-        load_q(0, 1)
-        load_mask(1)
+        cast_q(0, 0)
+        nc.scalar.dma_start(out=k_up[ROWS:, :], in_=k_mx[:ROWS, :])
+        nc.scalar.dma_start(out=k_down[:ROWS, :], in_=k_mx[ROWS:, :])
         load_q(1, 1)
         nc.sync.dma_start(
             out=v_raw[:].rearrange("p g j e -> p g (j e)"), in_=v.rearrange("g (p j) e -> p g (j e)", j=PACK)
         )
-        for c in range(2, CHUNKS):
-            load_q(0, c)
-            load_mask(c)
-            load_q(1, c)
-            load_og(c - 2)
-        load_og(CHUNKS - 2)
-        load_og(CHUNKS - 1)
+        load_og(0)
+        load_og(1)
+        load_og(3)
+        load_og(2)
 
-        quant_q(0, 0)
-        scores([0], 0)
-        make_mt(0)
-        cast_q(1, 0)
-        weigh(0, 0)
-        quant_q(1, 0)
-        scores([3], 0)
-        scores([1], 0)
-        scores([2], 0)
+        def cast_v():
+            nc.scalar.copy(
+                out=v_bf[:].rearrange("p g (c i) j -> p g c j i", i=4),
+                in_=v_raw[:].rearrange("p g j (c i) -> p g c j i", i=4),
+            )
+
+        def quant_v():
+            nc.vector.quantize_mx(
+                out=v_codes[:].bitcast(FP8X4), scales=v_scales[:], in_=v_bf[:].rearrange("p g e j -> p (g e j)")
+            )
+
         cast_q(0, 1)
-        make_mt(1)
-        weigh(3, 0)
-        cast_q(1, 1)
-        weigh(1, 0)
+        quant_q(0, 0)
+        scores(0, 0)
+        mt_vector(0)
         quant_q(0, 1)
-        scores([0, 1], 1)
-        weigh(2, 0)
-        quant_w(0, 0)
+        scores(0, 1)
+        cast_q(1, 0)
+        cast_q(1, 1)
+        cast_q(0, 2)
+        cast_q(0, 3)
+        scale_mask(1)
+        mt_scalar(2)
+        mt_scalar(3)
+        cast_q(1, 2)
+        cast_q(1, 3)
+        cast_v()
+        sigmoid(0)
+        sigmoid(1)
+        sigmoid(3)
+        sigmoid(2)
+        weigh(0, 0)
+        mt_vector(1)
+        quant_q(1, 0)
+        scores(3, 0)
+        weigh(0, 1)
         quant_q(1, 1)
-        scores([2, 3], 1)
-        nc.scalar.copy(
-            out=v_bf[:].rearrange("p g (c i) j -> p g c j i", i=4),
-            in_=v_raw[:].rearrange("p g j (c i) -> p g c j i", i=4),
-        )
-
-        for c in range(1, CHUNKS):
-            last = c == CHUNKS - 1
-            if not last:
-                cast_q(0, c + 1)
-                make_mt(c + 1)
-                cast_q(1, c + 1)
-            sigmoid(c - 1)
-            if last:
-                sigmoid(c)
-            weigh(0, c)
-            quant_w(1, c - 1)
-            weigh(1, c)
-            if c == 1:
-                nc.vector.quantize_mx(
-                    out=v_codes[:].bitcast(FP8X4), scales=v_scales[:], in_=v_bf[:].rearrange("p g e j -> p (g e j)")
-                )
-                values(0, 0)
-            values(1, c - 1)
-            if not last:
-                quant_q(0, c + 1)
-                scores([0, 1], c + 1)
-            weigh(2, c)
-            quant_w(0, c)
-            finish(c - 1, slice(0, H))
-            values(0, c)
-            weigh(3, c)
-            if not last:
-                quant_q(1, c + 1)
-                scores([2, 3], c + 1)
-        finish(CHUNKS - 1, slice(0, 2))
-        quant_w(1, CHUNKS - 1)
-        values(1, CHUNKS - 1)
-        finish(CHUNKS - 1, slice(2, H))
+        scores(3, 1)
+        scores(1, 0)
+        scores(2, 0)
+        quant_w(0, 0, 2)
+        weigh(3, 0)
+        scores(1, 1)
+        scores(2, 1)
+        weigh(3, 1)
+        weigh(1, 0)
+        quant_w(3, 0, 2)
+        quant_q(0, 2)
+        quant_q(0, 3)
+        weigh(2, 0)
+        scores(0, 2)
+        weigh(1, 1)
+        scores(1, 2)
+        scores(0, 3)
+        weigh(2, 1)
+        quant_w(1, 0, 2)
+        scores(1, 3)
+        weigh(0, 2)
+        quant_w(2, 0, 2)
+        weigh(1, 2)
+        weigh(0, 3)
+        quant_q(1, 2)
+        scores(3, 2)
+        scores(2, 2)
+        weigh(1, 3)
+        quant_w(0, 2, 4)
+        quant_q(1, 3)
+        scores(3, 3)
+        scores(2, 3)
+        weigh(3, 2)
+        quant_w(1, 2, 4)
+        quant_v()
+        values(0, 0, 4)
+        values(1, 0, 4)
+        weigh(3, 3)
+        weigh(2, 2)
+        quant_w(3, 2, 4)
+        finish(0, 0, 4)
+        values(2, 0, 2)
+        finish(1, 0, 4)
+        values(3, 0, 4)
+        weigh(2, 3)
+        quant_w(2, 2, 3)
+        finish(2, 0, 2)
+        quant_w(2, 3, 4)
+        values(2, 2, 4)
+        finish(3, 0, 4)
+        finish(2, 2, 4)

@@ -20,6 +20,7 @@ QC = 128
 CHUNKS = NQ // QC
 K_SPLIT = 84
 SCORE_BANKS = 3
+HEADS = ((1, 2), (0, 3))
 
 
 def tile_rows_a_relu_mask_gate_kernel(tc, qT, kT, t, v, mask, og, out):
@@ -36,28 +37,26 @@ def tile_rows_a_relu_mask_gate_kernel(tc, qT, kT, t, v, mask, og, out):
         warm = tile("warm", [P, 2], F32)
         k_raw = tile("k_raw", [P, PACK, N], F32)
         k_bf = tile("k_bf", [P, PACK, P, PACK], BF16)
-        k_mx = tile("k_mx", [P, N + N // 4], I32)
-        k_up = tile("k_up", [P, N + N // 4], I32)
-        k_down = tile("k_down", [P, N + N // 4], I32)
+        k_codes = tile("k_codes", [P, N], I32)
+        k_scales = tile("k_scales", [P, N], U8)
         v_raw = tile("v_raw", [P, KV, PACK, E], F32)
         v_bf = tile("v_bf", [P, KV, E, PACK], BF16)
         v_codes = tile("v_codes", [P, KV * E], I32)
         v_scales = tile("v_scales", [P, KV * E], U8)
-        pairs = [(a, c) for c in range(CHUNKS) for a in range(2)]
-        q_half = {(a, u): tile("q_half%d%d" % (a, u), [P, PACK, 2 * QC], F32) for a in range(2) for u in range(2)}
-        q_bf = {x: tile("q_bf%d%d" % x, [P, QC, PACK], BF16) for x in pairs}
-        q_codes = {x: tile("q_codes%d%d" % x, [P, QC], I32) for x in pairs}
-        q_scales = {x: tile("q_scales%d%d" % x, [P, QC], U8) for x in pairs}
-        halves = [(h, u) for h in range(H) for u in range(2)]
-        w_bf = {x: tile("w_bf%d%d" % x, [P, 2, QC, PACK], BF16) for x in halves}
-        w_codes = {x: tile("w_codes%d%d" % x, [P, 2 * QC], I32) for x in halves}
-        w_scales = {x: tile("w_scales%d%d" % x, [P, 2 * QC], U8) for x in halves}
+        halves = [(a, u) for a in range(2) for u in range(2)]
+        q_half = {x: tile("q_half%d%d" % x, [P, PACK, 2 * QC], F32) for x in halves}
+        q_bf = {x: tile("q_bf%d%d" % x, [P, 2, QC, PACK], BF16) for x in halves}
+        q_codes = {x: tile("q_codes%d%d" % x, [P, 2 * QC], I32) for x in halves}
+        q_scales = {x: tile("q_scales%d%d" % x, [P, 2 * QC], U8) for x in halves}
+        w_bf = {x: tile("w_bf%d%d" % x, [P, 4, QC, PACK], BF16) for x in halves}
+        w_codes = {x: tile("w_codes%d%d" % x, [P, 4 * QC], I32) for x in halves}
+        w_scales = {x: tile("w_scales%d%d" % x, [P, 4 * QC], U8) for x in halves}
         m_half = [tile("m_half%d" % u, [P, PACK, 2 * QC], F32) for u in range(2)]
-        m_scaled = tile("m_scaled", [P, PACK, 2 * QC], F32)
+        m_scaled = [tile("m_scaled%d" % c, [P, PACK, QC], F32) for c in range(CHUNKS)]
         mt = [tile("mt%d" % c, [P, QC, PACK], F32) for c in range(CHUNKS)]
         og_raw = [tile("og_raw%d" % h, [P, CHUNKS, E], F32) for h in range(H)]
-        gate = [tile("gate%d" % h, [P, CHUNKS, E], F32) for h in range(H)]
-        res = [tile("res%d" % h, [P, CHUNKS, E], F32) for h in range(H)]
+        gate = [tile("gate%d" % a, [P, 2, CHUNKS, E], F32) for a in range(2)]
+        res = [tile("res%d" % a, [P, 2, CHUNKS, E], F32) for a in range(2)]
         score_banks = [
             [ps.tile([P, PACK, QC], F32, name="score%d%d" % (g, b)) for b in range(SCORE_BANKS)] for g in range(2)
         ]
@@ -66,15 +65,20 @@ def tile_rows_a_relu_mask_gate_kernel(tc, qT, kT, t, v, mask, og, out):
         def cols(c):
             return slice(c * QC, (c + 1) * QC)
 
-        def q_rows(a):
-            return qT[2 * a : 2 * a + 2].rearrange("g (p j) q -> (g p) j q", j=PACK)
+        def half_cols(u):
+            return slice(2 * u * QC, 2 * (u + 1) * QC)
 
-        def load_q(a, u):
-            nc.sync.dma_start(out=q_half[a, u][:], in_=q_rows(a)[:, :, 2 * u * QC : 2 * (u + 1) * QC])
+        def load_q_adjacent(u):
+            rows = qT[1:3].rearrange("g (p j) q -> (g p) j q", j=PACK)
+            nc.sync.dma_start(out=q_half[0, u][:], in_=rows[:, :, half_cols(u)])
+
+        def load_q_outer(g, u, queue):
+            rows = qT[HEADS[1][g]].rearrange("(p j) q -> p j q", j=PACK)
+            queue.dma_start(out=q_half[1, u][ROWS * g : ROWS * (g + 1)], in_=rows[:, :, half_cols(u)])
 
         def load_mask(u):
             rows = mask.rearrange("(s r) q -> s r q", r=PACK)
-            nc.sync.dma_start(out=m_half[u][:], in_=rows[:, :, 2 * u * QC : 2 * (u + 1) * QC])
+            nc.sync.dma_start(out=m_half[u][:], in_=rows[:, :, half_cols(u)])
 
         def load_og(h):
             nc.sync.dma_start(out=og_raw[h][:], in_=og[h].rearrange("(c q) e -> q c e", q=QC))
@@ -82,15 +86,17 @@ def tile_rows_a_relu_mask_gate_kernel(tc, qT, kT, t, v, mask, og, out):
         def cast_q(a, c):
             raw = q_half[a, c // 2][:, :, cols(c % 2)]
             nc.scalar.copy(
-                out=q_bf[a, c][:].rearrange("p (c i) j -> p c j i", i=4),
+                out=q_bf[a, c // 2][:, c % 2].rearrange("p (c i) j -> p c j i", i=4),
                 in_=raw.rearrange("p j (c i) -> p c j i", i=4),
             )
 
-        def quant_q(a, c):
+        def quant_q(a, c0, c1):
+            u, x = divmod(c0, 2)
+            span = slice(x * QC, (x + c1 - c0) * QC)
             nc.vector.quantize_mx(
-                out=q_codes[a, c][:].bitcast(FP8X4),
-                scales=q_scales[a, c][:],
-                in_=q_bf[a, c][:].rearrange("p q j -> p (q j)"),
+                out=q_codes[a, u][:, span].bitcast(FP8X4),
+                scales=q_scales[a, u][:, span],
+                in_=q_bf[a, u][:, x : x + c1 - c0].rearrange("p c q j -> p (c q j)"),
             )
 
         def mt_vector(c):
@@ -101,120 +107,108 @@ def tile_rows_a_relu_mask_gate_kernel(tc, qT, kT, t, v, mask, og, out):
                 op=ALU.mult,
             )
 
-        def scale_mask(u):
+        def mt_scalar(c):
             for r in range(PACK):
                 nc.scalar.activation(
-                    out=m_scaled[:, r, :], in_=m_half[u][:, r, :], func=ACT.Copy, scale=t_sb[:, r : r + 1]
+                    out=m_scaled[c][:, r, :],
+                    in_=m_half[c // 2][:, r, cols(c % 2)],
+                    func=ACT.Copy,
+                    scale=t_sb[:, r : r + 1],
                 )
+            nc.scalar.copy(out=mt[c][:], in_=m_scaled[c][:].rearrange("p r q -> p q r"))
 
-        def mt_scalar(c):
-            nc.scalar.copy(out=mt[c][:], in_=m_scaled[:, :, cols(c % 2)].rearrange("p r q -> p q r"))
+        def bank(a, c, g):
+            return score_banks[g][(CHUNKS * a + c) % SCORE_BANKS]
 
-        bank_of = {}
-
-        def bank(h, c):
-            return bank_of[h, c]
-
-        def scores(h, c):
-            g = h % 2
-            bank_of[h, c] = score_banks[g][sum(1 for x in bank_of if x[0] % 2 == g) % SCORE_BANKS]
+        def score_pass(a, c, g, r):
             rows = slice(ROWS * g, ROWS * (g + 1))
-            keys = (k_mx, k_up, k_down, k_mx)[h]
-            for r in range(PACK):
-                nc.tensor.matmul_mx(
-                    out=bank(h, c)[:, r, :],
-                    lhsT=keys[rows, r * P : (r + 1) * P].bitcast(FP8X4),
-                    lhsT_scale=keys[rows, N:].bitcast(U8)[:, r * P : (r + 1) * P],
-                    rhs=q_codes[h // 2, c][rows, :].bitcast(FP8X4),
-                    rhs_scale=q_scales[h // 2, c][rows, :],
-                    start=True,
-                    stop=True,
-                )
+            nc.tensor.matmul_mx(
+                out=bank(a, c, g)[:, r, :],
+                lhsT=k_codes[rows, r * P : (r + 1) * P].bitcast(FP8X4),
+                lhsT_scale=k_scales[rows, r * P : (r + 1) * P],
+                rhs=q_codes[a, c // 2][rows, cols(c % 2)].bitcast(FP8X4),
+                rhs_scale=q_scales[a, c // 2][rows, cols(c % 2)],
+                start=True,
+                stop=True,
+            )
 
-        def weigh(h, c):
+        def scores(a, c):
+            for r in range(PACK):
+                for g in range(2):
+                    score_pass(a, c, g, r)
+
+        def scores_tile_by_tile(a, c):
+            for g in range(2):
+                for r in range(PACK):
+                    score_pass(a, c, g, r)
+
+        def weigh(a, c, g):
             nc.vector.scalar_tensor_tensor(
-                out=w_bf[h, c // 2][:, c % 2],
-                in0=bank(h, c)[:].rearrange("p r q -> p q r"),
+                out=w_bf[a, c // 2][:, 2 * (c % 2) + g],
+                in0=bank(a, c, g)[:].rearrange("p r q -> p q r"),
                 scalar=0.0,
                 in1=mt[c][:],
                 op0=ALU.max,
                 op1=ALU.mult,
             )
 
-        def quant_w(h, c0, c1):
-            u, x = divmod(c0, 2)
-            span = slice(x * QC, (x + c1 - c0) * QC)
+        def quant_w(a, u, s0, s1):
+            span = slice(s0 * QC, s1 * QC)
             nc.vector.quantize_mx(
-                out=w_codes[h, u][:, span].bitcast(FP8X4),
-                scales=w_scales[h, u][:, span],
-                in_=w_bf[h, u][:, x : x + c1 - c0].rearrange("p c q r -> p (c q r)"),
+                out=w_codes[a, u][:, span].bitcast(FP8X4),
+                scales=w_scales[a, u][:, span],
+                in_=w_bf[a, u][:, s0:s1].rearrange("p s q r -> p (s q r)"),
             )
 
-        def y_slot(h, c0, c1):
-            b = h % 2
-            return y_banks[b][:, c0:c1]
+        def values(a, c, g, y):
+            s = 2 * (c % 2) + g
+            nc.tensor.matmul_mx(
+                out=y,
+                lhsT=w_codes[a, c // 2][:, cols(s)].bitcast(FP8X4),
+                lhsT_scale=w_scales[a, c // 2][:, cols(s)],
+                rhs=v_codes[:, cols(g)].bitcast(FP8X4),
+                rhs_scale=v_scales[:, cols(g)],
+                start=True,
+                stop=True,
+            )
 
-        def values(h, c0, c1):
-            for c in range(c0, c1):
-                u, x = divmod(c, 2)
-                nc.tensor.matmul_mx(
-                    out=y_slot(h, c, c + 1)[:, 0, :],
-                    lhsT=w_codes[h, u][:, x * QC : (x + 1) * QC].bitcast(FP8X4),
-                    lhsT_scale=w_scales[h, u][:, x * QC : (x + 1) * QC],
-                    rhs=v_codes[:, (h // 2) * E : (h // 2 + 1) * E].bitcast(FP8X4),
-                    rhs_scale=v_scales[:, (h // 2) * E : (h // 2 + 1) * E],
-                    start=True,
-                    stop=True,
-                )
+        def sigmoid(a, g):
+            nc.scalar.activation(out=gate[a][:, g], in_=og_raw[HEADS[a][g]][:], func=ACT.Sigmoid)
 
-        def sigmoid(h):
-            nc.scalar.activation(out=gate[h][:], in_=og_raw[h][:], func=ACT.Sigmoid)
-
-        def store(h, c0, c1):
-            nc.sync.dma_start(out=out[h].rearrange("(c q) e -> q c e", q=QC)[:, c0:c1], in_=res[h][:, c0:c1])
-
-        def finish(h, c0, c1):
+        def finish(a, gs, c0, c1, y):
             nc.vector.scalar_tensor_tensor(
-                out=res[h][:, c0:c1],
-                in0=y_slot(h, c0, c1),
+                out=res[a][:, gs, c0:c1].rearrange("p g c e -> p g (c e)"),
+                in0=y,
                 scalar=1.0 / 16.0,
-                in1=gate[h][:, c0:c1],
+                in1=gate[a][:, gs, c0:c1].rearrange("p g c e -> p g (c e)"),
                 op0=ALU.mult,
                 op1=ALU.mult,
             )
-            store(h, c0, c1)
 
-        nc.sync.dma_start(out=k_raw[:], in_=kT.rearrange("g (p j) n -> (g p) j n", j=PACK))
-        nc.scalar.dma_start(out=t_sb[:], in_=t.rearrange("(s r) o -> s (r o)", r=PACK))
-        load_q(0, 0)
-        load_mask(0)
-        load_q(1, 0)
-        load_q(0, 1)
-        load_mask(1)
-        nc.vector.memset(warm[:, 0:1], 0.0)
-        nc.vector.memset(k_mx[:, N:], 0)
-        nc.scalar.activation(out=warm[:, 1:2], in_=warm[:, 0:1], func=ACT.Sigmoid)
+        def store_head(a, g, c0, c1):
+            rows = out[HEADS[a][g]].rearrange("(c q) e -> q c e", q=QC)
+            nc.sync.dma_start(out=rows[:, c0:c1], in_=res[a][:, g, c0:c1])
 
-        k_src = k_raw[:].rearrange("p j (s r) -> p s r j", r=PACK)
-        k_dst = k_bf[:].rearrange("p r s j -> p s r j")
-        nc.vector.tensor_copy(out=k_dst[:, :K_SPLIT], in_=k_src[:, :K_SPLIT])
-        nc.scalar.copy(out=k_dst[:, K_SPLIT:], in_=k_src[:, K_SPLIT:])
-        nc.vector.quantize_mx(
-            out=k_mx[:, :N].bitcast(FP8X4),
-            scales=k_mx[:, N:].bitcast(U8),
-            in_=k_bf[:].rearrange("p r s j -> p (r s j)"),
-        )
-        cast_q(0, 0)
-        nc.scalar.dma_start(out=k_up[ROWS:, :], in_=k_mx[:ROWS, :])
-        nc.scalar.dma_start(out=k_down[:ROWS, :], in_=k_mx[ROWS:, :])
-        load_q(1, 1)
-        nc.sync.dma_start(
-            out=v_raw[:].rearrange("p g j e -> p g (j e)"), in_=v.rearrange("g (p j) e -> p g (j e)", j=PACK)
-        )
-        load_og(0)
-        load_og(1)
-        load_og(3)
-        load_og(2)
+        def store_outer_chunk(c):
+            rows = out[0:4:3, cols(c)].rearrange("g q e -> q g e")
+            nc.sync.dma_start(out=rows, in_=res[1][:, :, c])
+
+        def values_head(g, b):
+            for c in range(CHUNKS):
+                values(0, c, g, y_banks[b][:, c])
+
+        def finish_head(g, b):
+            finish(0, slice(g, g + 1), 0, CHUNKS, y_banks[b][:].rearrange("p (g c) e -> p g (c e)", g=1))
+            store_head(0, g, 0, CHUNKS)
+
+        def values_outer(c0, c1, b):
+            for g in range(2):
+                for c in range(c0, c1):
+                    values(1, c, g, y_banks[b][:, g * (c1 - c0) + c - c0])
+
+        def finish_outer(c0, c1, b):
+            y = y_banks[b][:, : 2 * (c1 - c0)].rearrange("p (g c) e -> p g (c e)", g=2)
+            finish(1, slice(0, 2), c0, c1, y)
 
         def cast_v():
             nc.scalar.copy(
@@ -227,80 +221,102 @@ def tile_rows_a_relu_mask_gate_kernel(tc, qT, kT, t, v, mask, og, out):
                 out=v_codes[:].bitcast(FP8X4), scales=v_scales[:], in_=v_bf[:].rearrange("p g e j -> p (g e j)")
             )
 
+        def load_v():
+            nc.sync.dma_start(
+                out=v_raw[:].rearrange("p g j e -> p g (j e)"), in_=v.rearrange("g (p j) e -> p g (j e)", j=PACK)
+            )
+
+        def keys():
+            k_src = k_raw[:].rearrange("p j (s r) -> p s r j", r=PACK)
+            k_dst = k_bf[:].rearrange("p r s j -> p s r j")
+            nc.vector.tensor_copy(out=k_dst[:, :K_SPLIT], in_=k_src[:, :K_SPLIT])
+            nc.scalar.copy(out=k_dst[:, K_SPLIT:], in_=k_src[:, K_SPLIT:])
+            nc.vector.quantize_mx(
+                out=k_codes[:].bitcast(FP8X4), scales=k_scales[:], in_=k_bf[:].rearrange("p r s j -> p (r s j)")
+            )
+
+        nc.sync.dma_start(out=k_raw[:], in_=kT.rearrange("g (p j) n -> (g p) j n", j=PACK))
+        nc.scalar.dma_start(out=t_sb[:], in_=t.rearrange("(s r) o -> s (r o)", r=PACK))
+        load_q_adjacent(0)
+        load_mask(0)
+        load_q_adjacent(1)
+        load_mask(1)
+        load_q_outer(0, 0, nc.sync)
+        load_q_outer(1, 0, nc.sync)
+        nc.vector.memset(warm[:, 0:1], 0.0)
+        nc.scalar.activation(out=warm[:, 1:2], in_=warm[:, 0:1], func=ACT.Sigmoid)
+        load_q_outer(0, 1, nc.sync)
+        load_q_outer(1, 1, nc.sync)
+        load_v()
+        load_og(1)
+        load_og(2)
+        load_og(0)
+        load_og(3)
+        keys()
+        cast_q(0, 0)
         cast_q(0, 1)
-        quant_q(0, 0)
-        scores(0, 0)
-        mt_vector(0)
-        quant_q(0, 1)
+        quant_q(0, 0, 1)
+        scores_tile_by_tile(0, 0)
+        quant_q(0, 1, 2)
         scores(0, 1)
-        cast_q(1, 0)
-        cast_q(1, 1)
+        mt_vector(0)
+        mt_scalar(1)
         cast_q(0, 2)
         cast_q(0, 3)
-        scale_mask(1)
         mt_scalar(2)
         mt_scalar(3)
+        cast_q(1, 0)
+        cast_q(1, 1)
         cast_q(1, 2)
         cast_q(1, 3)
         cast_v()
-        sigmoid(0)
-        sigmoid(1)
-        sigmoid(3)
-        sigmoid(2)
-        weigh(0, 0)
-        mt_vector(1)
-        quant_q(1, 0)
-        scores(3, 0)
-        weigh(0, 1)
-        quant_q(1, 1)
-        scores(3, 1)
-        scores(1, 0)
-        scores(2, 0)
-        quant_w(0, 0, 2)
-        weigh(3, 0)
-        scores(1, 1)
-        scores(2, 1)
-        weigh(3, 1)
-        weigh(1, 0)
-        quant_w(3, 0, 2)
-        quant_q(0, 2)
-        quant_q(0, 3)
-        weigh(2, 0)
+        sigmoid(0, 0)
+        sigmoid(0, 1)
+        sigmoid(1, 0)
+        sigmoid(1, 1)
+        weigh(0, 0, 0)
+        weigh(0, 0, 1)
+        weigh(0, 1, 0)
+        quant_q(0, 2, 4)
         scores(0, 2)
-        weigh(1, 1)
-        scores(1, 2)
         scores(0, 3)
-        weigh(2, 1)
-        quant_w(1, 0, 2)
-        scores(1, 3)
-        weigh(0, 2)
-        quant_w(2, 0, 2)
-        weigh(1, 2)
-        weigh(0, 3)
-        quant_q(1, 2)
-        scores(3, 2)
-        scores(2, 2)
-        weigh(1, 3)
-        quant_w(0, 2, 4)
-        quant_q(1, 3)
-        scores(3, 3)
-        scores(2, 3)
-        weigh(3, 2)
-        quant_w(1, 2, 4)
+        weigh(0, 1, 1)
+        quant_w(0, 0, 0, 4)
+        weigh(0, 2, 0)
+        weigh(0, 2, 1)
+        weigh(0, 3, 0)
+        quant_q(1, 0, 1)
+        scores(1, 0)
+        weigh(0, 3, 1)
+        quant_q(1, 1, 2)
+        scores(1, 1)
+        quant_w(0, 1, 0, 4)
+        weigh(1, 0, 0)
+        weigh(1, 0, 1)
+        quant_q(1, 2, 4)
+        scores(1, 2)
+        weigh(1, 1, 0)
         quant_v()
-        values(0, 0, 4)
-        values(1, 0, 4)
-        weigh(3, 3)
-        weigh(2, 2)
-        quant_w(3, 2, 4)
-        finish(0, 0, 4)
-        values(2, 0, 2)
-        finish(1, 0, 4)
-        values(3, 0, 4)
-        weigh(2, 3)
-        quant_w(2, 2, 3)
-        finish(2, 0, 2)
-        quant_w(2, 3, 4)
-        values(2, 2, 4)
-        finish(3, 0, 4)
-        finish(2, 2, 4)
+        values_head(0, 0)
+        values_head(1, 1)
+        weigh(1, 1, 1)
+        scores(1, 3)
+        finish_head(0, 0)
+        quant_w(1, 0, 0, 4)
+        values_outer(0, 2, 0)
+        finish_head(1, 1)
+        weigh(1, 2, 0)
+        weigh(1, 2, 1)
+        weigh(1, 3, 0)
+        quant_w(1, 1, 0, 2)
+        values_outer(2, 3, 1)
+        weigh(1, 3, 1)
+        finish_outer(0, 2, 0)
+        store_head(1, 0, 0, 2)
+        store_head(1, 1, 0, 2)
+        quant_w(1, 1, 2, 4)
+        values_outer(3, 4, 0)
+        finish_outer(2, 3, 1)
+        store_outer_chunk(2)
+        finish_outer(3, 4, 0)
+        store_outer_chunk(3)

@@ -107,7 +107,7 @@ def tile_rows_a_relu_mask_gate_kernel(tc, qT, kT, t, v, mask, og, out):
                 op=ALU.mult,
             )
 
-        def mt_scalar(c):
+        def scale_mask(c):
             for r in range(PACK):
                 nc.scalar.activation(
                     out=m_scaled[c][:, r, :],
@@ -115,6 +115,8 @@ def tile_rows_a_relu_mask_gate_kernel(tc, qT, kT, t, v, mask, og, out):
                     func=ACT.Copy,
                     scale=t_sb[:, r : r + 1],
                 )
+
+        def weave_mask(c):
             nc.scalar.copy(out=mt[c][:], in_=m_scaled[c][:].rearrange("p r q -> p q r"))
 
         def bank(a, c, g):
@@ -210,6 +212,13 @@ def tile_rows_a_relu_mask_gate_kernel(tc, qT, kT, t, v, mask, og, out):
             y = y_banks[b][:, : 2 * (c1 - c0)].rearrange("p (g c) e -> p g (c e)", g=2)
             finish(1, slice(0, 2), c0, c1, y)
 
+        def values_last(g, b):
+            values(1, CHUNKS - 1, g, y_banks[b][:, 0])
+
+        def finish_last(g, b):
+            finish(1, slice(g, g + 1), CHUNKS - 1, CHUNKS, y_banks[b][:, 0:1])
+            store_head(1, g, CHUNKS - 1, CHUNKS)
+
         def cast_v():
             nc.scalar.copy(
                 out=v_bf[:].rearrange("p g (c i) j -> p g c j i", i=4),
@@ -245,9 +254,9 @@ def tile_rows_a_relu_mask_gate_kernel(tc, qT, kT, t, v, mask, og, out):
         load_q_outer(1, 0, nc.sync)
         nc.vector.memset(warm[:, 0:1], 0.0)
         nc.scalar.activation(out=warm[:, 1:2], in_=warm[:, 0:1], func=ACT.Sigmoid)
+        load_v()
         load_q_outer(0, 1, nc.sync)
         load_q_outer(1, 1, nc.sync)
-        load_v()
         load_og(1)
         load_og(2)
         load_og(0)
@@ -257,19 +266,20 @@ def tile_rows_a_relu_mask_gate_kernel(tc, qT, kT, t, v, mask, og, out):
         cast_q(0, 1)
         quant_q(0, 0, 1)
         scores_tile_by_tile(0, 0)
+        mt_vector(0)
         quant_q(0, 1, 2)
         scores(0, 1)
-        mt_vector(0)
-        mt_scalar(1)
+        scale_mask(1)
+        weave_mask(1)
         cast_q(0, 2)
         cast_q(0, 3)
-        mt_scalar(2)
-        mt_scalar(3)
+        scale_mask(3)
+        weave_mask(3)
         cast_q(1, 0)
         cast_q(1, 1)
+        cast_v()
         cast_q(1, 2)
         cast_q(1, 3)
-        cast_v()
         sigmoid(0, 0)
         sigmoid(0, 1)
         sigmoid(1, 0)
@@ -277,46 +287,52 @@ def tile_rows_a_relu_mask_gate_kernel(tc, qT, kT, t, v, mask, og, out):
         weigh(0, 0, 0)
         weigh(0, 0, 1)
         weigh(0, 1, 0)
-        quant_q(0, 2, 4)
+        quant_q(0, 2, 3)
         scores(0, 2)
-        scores(0, 3)
         weigh(0, 1, 1)
+        quant_q(0, 3, 4)
+        scores(0, 3)
+        mt_vector(2)
         quant_w(0, 0, 0, 4)
         weigh(0, 2, 0)
         weigh(0, 2, 1)
         weigh(0, 3, 0)
         quant_q(1, 0, 1)
-        scores(1, 0)
+        scores_tile_by_tile(1, 0)
         weigh(0, 3, 1)
         quant_q(1, 1, 2)
         scores(1, 1)
         quant_w(0, 1, 0, 4)
         weigh(1, 0, 0)
-        weigh(1, 0, 1)
-        quant_q(1, 2, 4)
-        scores(1, 2)
-        weigh(1, 1, 0)
         quant_v()
         values_head(0, 0)
         values_head(1, 1)
+        weigh(1, 0, 1)
+        weigh(1, 1, 0)
         weigh(1, 1, 1)
+        quant_q(1, 2, 4)
+        scores(1, 2)
         scores(1, 3)
-        finish_head(0, 0)
         quant_w(1, 0, 0, 4)
-        values_outer(0, 2, 0)
+        finish_head(0, 0)
+        values_outer(0, 1, 0)
         finish_head(1, 1)
+        values_outer(1, 2, 1)
         weigh(1, 2, 0)
         weigh(1, 2, 1)
         weigh(1, 3, 0)
+        finish_outer(0, 1, 0)
+        store_outer_chunk(0)
         quant_w(1, 1, 0, 2)
-        values_outer(2, 3, 1)
+        values_outer(2, 3, 0)
         weigh(1, 3, 1)
-        finish_outer(0, 2, 0)
-        store_head(1, 0, 0, 2)
-        store_head(1, 1, 0, 2)
-        quant_w(1, 1, 2, 4)
-        values_outer(3, 4, 0)
-        finish_outer(2, 3, 1)
+        quant_w(1, 1, 2, 3)
+        finish_outer(2, 3, 0)
         store_outer_chunk(2)
-        finish_outer(3, 4, 0)
-        store_outer_chunk(3)
+        values_last(0, 0)
+        quant_w(1, 1, 3, 4)
+        finish_outer(1, 2, 1)
+        store_outer_chunk(1)
+        values_last(1, 1)
+        finish_last(0, 0)
+        finish_last(1, 1)

@@ -268,7 +268,7 @@ def tile_rows_a_relu_mask_gate_kernel(tc, qT, kT, t, v, mask, og, out):
         scores_tile_by_tile(0, 0)
         mt_vector(0)
         quant_q(0, 1, 2)
-        scores(0, 1)
+        scores_tile_by_tile(0, 1)
         scale_mask(1)
         weave_mask(1)
         cast_q(0, 2)
@@ -288,10 +288,10 @@ def tile_rows_a_relu_mask_gate_kernel(tc, qT, kT, t, v, mask, og, out):
         weigh(0, 0, 1)
         weigh(0, 1, 0)
         quant_q(0, 2, 3)
-        scores(0, 2)
+        scores_tile_by_tile(0, 2)
         weigh(0, 1, 1)
         quant_q(0, 3, 4)
-        scores(0, 3)
+        scores_tile_by_tile(0, 3)
         mt_vector(2)
         quant_w(0, 0, 0, 4)
         weigh(0, 2, 0)
@@ -301,20 +301,21 @@ def tile_rows_a_relu_mask_gate_kernel(tc, qT, kT, t, v, mask, og, out):
         scores_tile_by_tile(1, 0)
         weigh(0, 3, 1)
         quant_q(1, 1, 2)
-        scores(1, 1)
+        scores_tile_by_tile(1, 1)
         quant_w(0, 1, 0, 4)
-        weigh(1, 0, 0)
         quant_v()
         values_head(0, 0)
         values_head(1, 1)
+        weigh(1, 0, 0)
         weigh(1, 0, 1)
         weigh(1, 1, 0)
+        quant_q(1, 2, 3)
+        scores_tile_by_tile(1, 2)
         weigh(1, 1, 1)
-        quant_q(1, 2, 4)
-        scores(1, 2)
-        scores(1, 3)
-        quant_w(1, 0, 0, 4)
+        quant_q(1, 3, 4)
+        scores_tile_by_tile(1, 3)
         finish_head(0, 0)
+        quant_w(1, 0, 0, 4)
         values_outer(0, 1, 0)
         finish_head(1, 1)
         values_outer(1, 2, 1)

@@ -17,10 +17,11 @@ P = 128
 ROWS = 64
 PACK = 4
 QC = 128
-CHUNKS = NQ // QC
 K_SPLIT = 84
 SCORE_BANKS = 3
 HEADS = ((1, 2), (0, 3))
+HEAD_SLICE = (slice(1, 3), slice(0, 4, 3))
+PIECES = ((0, 1), (128, 1), (256, 2))
 
 
 def tile_rows_a_relu_mask_gate_kernel(tc, qT, kT, t, v, mask, og, out):
@@ -43,181 +44,190 @@ def tile_rows_a_relu_mask_gate_kernel(tc, qT, kT, t, v, mask, og, out):
         v_bf = tile("v_bf", [P, KV, E, PACK], BF16)
         v_codes = tile("v_codes", [P, KV * E], I32)
         v_scales = tile("v_scales", [P, KV * E], U8)
-        halves = [(a, u) for a in range(2) for u in range(2)]
-        q_half = {x: tile("q_half%d%d" % x, [P, PACK, 2 * QC], F32) for x in halves}
-        q_bf = {x: tile("q_bf%d%d" % x, [P, 2, QC, PACK], BF16) for x in halves}
-        q_codes = {x: tile("q_codes%d%d" % x, [P, 2 * QC], I32) for x in halves}
-        q_scales = {x: tile("q_scales%d%d" % x, [P, 2 * QC], U8) for x in halves}
-        w_bf = {x: tile("w_bf%d%d" % x, [P, 4, QC, PACK], BF16) for x in halves}
-        w_codes = {x: tile("w_codes%d%d" % x, [P, 4 * QC], I32) for x in halves}
-        w_scales = {x: tile("w_scales%d%d" % x, [P, 4 * QC], U8) for x in halves}
-        m_half = [tile("m_half%d" % u, [P, PACK, 2 * QC], F32) for u in range(2)]
-        m_scaled = [tile("m_scaled%d" % c, [P, PACK, QC], F32) for c in range(CHUNKS)]
-        mt = [tile("mt%d" % c, [P, QC, PACK], F32) for c in range(CHUNKS)]
-        og_raw = [tile("og_raw%d" % h, [P, CHUNKS, E], F32) for h in range(H)]
-        gate = [tile("gate%d" % a, [P, 2, CHUNKS, E], F32) for a in range(2)]
-        res = [tile("res%d" % a, [P, 2, CHUNKS, E], F32) for a in range(2)]
+        width = [n for q0, n in PIECES]
+        both = [(a, i) for a in range(2) for i in range(len(PIECES))]
+        q_raw = {x: tile("q_raw%d%d" % x, [P, PACK, width[x[1]] * QC], F32) for x in both if x > (0, 1)}
+        q_first = tile("q_first", [P, PACK, 2 * QC], F32)
+        q_raw[0, 0] = q_first[:, :, :QC]
+        q_raw[0, 1] = q_first[:, :, QC:]
+        q_bf = {x: tile("q_bf%d%d" % x, [P, width[x[1]], QC, PACK], BF16) for x in both}
+        q_codes = {x: tile("q_codes%d%d" % x, [P, width[x[1]] * QC], I32) for x in both}
+        q_scales = {x: tile("q_scales%d%d" % x, [P, width[x[1]] * QC], U8) for x in both}
+        w_bf = {x: tile("w_bf%d%d" % x, [P, 2 * width[x[1]], QC, PACK], BF16) for x in both}
+        w_codes = {x: tile("w_codes%d%d" % x, [P, 2 * width[x[1]] * QC], I32) for x in both}
+        w_scales = {x: tile("w_scales%d%d" % x, [P, 2 * width[x[1]] * QC], U8) for x in both}
+        og_raw = [tile("og_raw%d" % i, [P, H, n * E], F32) for i, n in enumerate(width)]
+        gate = [tile("gate%d" % i, [P, H, n * E], F32) for i, n in enumerate(width)]
+        res = [tile("res%d" % i, [P, H, n * E], F32) for i, n in enumerate(width)]
+        m_raw = [tile("m_raw%d" % u, [P, PACK, 2 * QC], F32) for u in range(2)]
+        m_scaled = {(i, e): tile("m_scaled%d%d" % (i, e), [P, PACK, QC], F32) for i in (1, 2) for e in range(width[i])}
+        mt = {(i, e): tile("mt%d%d" % (i, e), [P, QC, PACK], F32) for i in range(3) for e in range(width[i])}
         score_banks = [
             [ps.tile([P, PACK, QC], F32, name="score%d%d" % (g, b)) for b in range(SCORE_BANKS)] for g in range(2)
         ]
-        y_banks = [ps.tile([P, CHUNKS, E], F32, name="y%d" % b) for b in range(2)]
+        y_banks = [ps.tile([P, PACK * E], F32, name="y%d" % b) for b in range(2)]
 
         def cols(c):
             return slice(c * QC, (c + 1) * QC)
 
-        def half_cols(u):
-            return slice(2 * u * QC, 2 * (u + 1) * QC)
+        def span(i):
+            return slice(PIECES[i][0], PIECES[i][0] + width[i] * QC)
 
-        def load_q_adjacent(u):
+        def load_q(a, i):
+            if a == 0:
+                rows = qT[1:3].rearrange("g (p j) q -> (g p) j q", j=PACK)
+                nc.sync.dma_start(out=q_raw[a, i][:], in_=rows[:, :, span(i)])
+            else:
+                for g in range(2):
+                    rows = qT[HEADS[a][g]].rearrange("(p j) q -> p j q", j=PACK)
+                    nc.sync.dma_start(out=q_raw[a, i][ROWS * g : ROWS * (g + 1)], in_=rows[:, :, span(i)])
+
+        def load_q_first():
             rows = qT[1:3].rearrange("g (p j) q -> (g p) j q", j=PACK)
-            nc.sync.dma_start(out=q_half[0, u][:], in_=rows[:, :, half_cols(u)])
-
-        def load_q_outer(g, u, queue):
-            rows = qT[HEADS[1][g]].rearrange("(p j) q -> p j q", j=PACK)
-            queue.dma_start(out=q_half[1, u][ROWS * g : ROWS * (g + 1)], in_=rows[:, :, half_cols(u)])
+            nc.sync.dma_start(out=q_first[:], in_=rows[:, :, : 2 * QC])
 
         def load_mask(u):
             rows = mask.rearrange("(s r) q -> s r q", r=PACK)
-            nc.sync.dma_start(out=m_half[u][:], in_=rows[:, :, half_cols(u)])
+            nc.sync.dma_start(out=m_raw[u][:], in_=rows[:, :, 2 * u * QC : 2 * (u + 1) * QC])
 
-        def load_og(h):
-            nc.sync.dma_start(out=og_raw[h][:], in_=og[h].rearrange("(c q) e -> q c e", q=QC))
+        def mask_of(i, e):
+            u, first = divmod(PIECES[i][0], 2 * QC)
+            return m_raw[u][:, :, first + e : first + width[i] * QC : width[i]]
 
-        def cast_q(a, c):
-            raw = q_half[a, c // 2][:, :, cols(c % 2)]
+        def dealt(x, i):
+            return x[:, span(i)].rearrange("h (m e) f -> m h (e f)", m=QC)
+
+        def load_og(i, heads):
+            nc.sync.dma_start(out=og_raw[i][:, heads], in_=dealt(og, i)[:, heads])
+
+        def load_v():
+            nc.sync.dma_start(
+                out=v_raw[:].rearrange("p g j e -> p g (j e)"), in_=v.rearrange("g (p j) e -> p g (j e)", j=PACK)
+            )
+
+        def cast_q(a, i, e, copy):
+            n = width[i]
+            copy(
+                out=q_bf[a, i][:, e].rearrange("p (c i) j -> p c j i", i=4 // n),
+                in_=q_raw[a, i][:, :, e::n].rearrange("p j (c i) -> p c j i", i=4 // n),
+            )
+
+        def cast_q_both(a, i):
             nc.scalar.copy(
-                out=q_bf[a, c // 2][:, c % 2].rearrange("p (c i) j -> p c j i", i=4),
-                in_=raw.rearrange("p j (c i) -> p c j i", i=4),
+                out=q_bf[a, i][:].rearrange("p e (c i) j -> p c j i e", i=2),
+                in_=q_raw[a, i][:].rearrange("p j (c i e) -> p c j i e", i=2, e=2),
             )
 
-        def quant_q(a, c0, c1):
-            u, x = divmod(c0, 2)
-            span = slice(x * QC, (x + c1 - c0) * QC)
+        def quant_q(a, i, e0, e1):
+            part = slice(e0 * QC, e1 * QC)
             nc.vector.quantize_mx(
-                out=q_codes[a, u][:, span].bitcast(FP8X4),
-                scales=q_scales[a, u][:, span],
-                in_=q_bf[a, u][:, x : x + c1 - c0].rearrange("p c q j -> p (c q j)"),
+                out=q_codes[a, i][:, part].bitcast(FP8X4),
+                scales=q_scales[a, i][:, part],
+                in_=q_bf[a, i][:, e0:e1].rearrange("p e q j -> p (e q j)"),
             )
 
-        def mt_vector(c):
+        def mt_vector(i, e):
             nc.vector.tensor_tensor(
-                out=mt[c][:],
-                in0=m_half[c // 2][:, :, cols(c % 2)].rearrange("p r q -> p q r"),
-                in1=t_sb[:, 0:PACK].unsqueeze(1).to_broadcast([P, QC, PACK]),
+                out=mt[i, e][:].rearrange("p (c i) r -> p c r i", i=2),
+                in0=mask_of(i, e).rearrange("p r (c i) -> p c r i", i=2),
+                in1=t_sb[:, 0:PACK].unsqueeze(1).unsqueeze(3).to_broadcast([P, QC // 2, PACK, 2]),
                 op=ALU.mult,
             )
 
-        def scale_mask(c):
+        def scale_mask(i, e):
             for r in range(PACK):
                 nc.scalar.activation(
-                    out=m_scaled[c][:, r, :],
-                    in_=m_half[c // 2][:, r, cols(c % 2)],
+                    out=m_scaled[i, e][:, r, :],
+                    in_=mask_of(i, e)[:, r],
                     func=ACT.Copy,
                     scale=t_sb[:, r : r + 1],
                 )
 
-        def weave_mask(c):
-            nc.scalar.copy(out=mt[c][:], in_=m_scaled[c][:].rearrange("p r q -> p q r"))
-
-        def bank(a, c, g):
-            return score_banks[g][(CHUNKS * a + c) % SCORE_BANKS]
-
-        def score_pass(a, c, g, r):
-            rows = slice(ROWS * g, ROWS * (g + 1))
-            nc.tensor.matmul_mx(
-                out=bank(a, c, g)[:, r, :],
-                lhsT=k_codes[rows, r * P : (r + 1) * P].bitcast(FP8X4),
-                lhsT_scale=k_scales[rows, r * P : (r + 1) * P],
-                rhs=q_codes[a, c // 2][rows, cols(c % 2)].bitcast(FP8X4),
-                rhs_scale=q_scales[a, c // 2][rows, cols(c % 2)],
-                start=True,
-                stop=True,
+        def weave_mask(i, e):
+            nc.scalar.copy(
+                out=mt[i, e][:].rearrange("p (c i) r -> p c r i", i=2),
+                in_=m_scaled[i, e][:].rearrange("p r (c i) -> p c r i", i=2),
             )
 
-        def scores(a, c):
+        turn = [0, 0]
+        held = {}
+
+        def scores(a, i, e, g):
+            rows = slice(ROWS * g, ROWS * (g + 1))
+            bank = score_banks[g][turn[g] % SCORE_BANKS]
+            turn[g] = turn[g] + 1
+            held[a, i, e, g] = bank
             for r in range(PACK):
-                for g in range(2):
-                    score_pass(a, c, g, r)
+                nc.tensor.matmul_mx(
+                    out=bank[:, r, :],
+                    lhsT=k_codes[rows, r * P : (r + 1) * P].bitcast(FP8X4),
+                    lhsT_scale=k_scales[rows, r * P : (r + 1) * P],
+                    rhs=q_codes[a, i][rows, cols(e)].bitcast(FP8X4),
+                    rhs_scale=q_scales[a, i][rows, cols(e)],
+                    start=True,
+                    stop=True,
+                )
 
-        def scores_tile_by_tile(a, c):
-            for g in range(2):
-                for r in range(PACK):
-                    score_pass(a, c, g, r)
-
-        def weigh(a, c, g):
+        def weigh(a, i, e, g):
             nc.vector.scalar_tensor_tensor(
-                out=w_bf[a, c // 2][:, 2 * (c % 2) + g],
-                in0=bank(a, c, g)[:].rearrange("p r q -> p q r"),
+                out=w_bf[a, i][:, g * width[i] + e],
+                in0=held[a, i, e, g][:].rearrange("p r q -> p q r"),
                 scalar=0.0,
-                in1=mt[c][:],
+                in1=mt[i, e][:],
                 op0=ALU.max,
                 op1=ALU.mult,
             )
 
-        def quant_w(a, u, s0, s1):
-            span = slice(s0 * QC, s1 * QC)
+        def quant_w(a, i, s0, s1):
+            part = slice(s0 * QC, s1 * QC)
             nc.vector.quantize_mx(
-                out=w_codes[a, u][:, span].bitcast(FP8X4),
-                scales=w_scales[a, u][:, span],
-                in_=w_bf[a, u][:, s0:s1].rearrange("p s q r -> p (s q r)"),
+                out=w_codes[a, i][:, part].bitcast(FP8X4),
+                scales=w_scales[a, i][:, part],
+                in_=w_bf[a, i][:, s0:s1].rearrange("p s q r -> p (s q r)"),
             )
 
-        def values(a, c, g, y):
-            s = 2 * (c % 2) + g
+        def value_pass(a, i, s, y):
+            g = s // width[i]
             nc.tensor.matmul_mx(
                 out=y,
-                lhsT=w_codes[a, c // 2][:, cols(s)].bitcast(FP8X4),
-                lhsT_scale=w_scales[a, c // 2][:, cols(s)],
+                lhsT=w_codes[a, i][:, cols(s)].bitcast(FP8X4),
+                lhsT_scale=w_scales[a, i][:, cols(s)],
                 rhs=v_codes[:, cols(g)].bitcast(FP8X4),
                 rhs_scale=v_scales[:, cols(g)],
                 start=True,
                 stop=True,
             )
 
-        def sigmoid(a, g):
-            nc.scalar.activation(out=gate[a][:, g], in_=og_raw[HEADS[a][g]][:], func=ACT.Sigmoid)
+        def values_chunk(i, b):
+            for a in range(2):
+                for g in range(2):
+                    value_pass(a, i, g, y_banks[b][:, cols(HEADS[a][g])])
 
-        def finish(a, gs, c0, c1, y):
-            nc.vector.scalar_tensor_tensor(
-                out=res[a][:, gs, c0:c1].rearrange("p g c e -> p g (c e)"),
-                in0=y,
-                scalar=1.0 / 16.0,
-                in1=gate[a][:, gs, c0:c1].rearrange("p g c e -> p g (c e)"),
-                op0=ALU.mult,
-                op1=ALU.mult,
-            )
+        def values(a, i, s0, s1, b):
+            for s in range(s0, s1):
+                value_pass(a, i, s, y_banks[b][:, cols(s)])
 
-        def store_head(a, g, c0, c1):
-            rows = out[HEADS[a][g]].rearrange("(c q) e -> q c e", q=QC)
-            nc.sync.dma_start(out=rows[:, c0:c1], in_=res[a][:, g, c0:c1])
+        def sigmoid(i, heads):
+            nc.scalar.activation(out=gate[i][:, heads], in_=og_raw[i][:, heads], func=ACT.Sigmoid)
 
-        def store_outer_chunk(c):
-            rows = out[0:4:3, cols(c)].rearrange("g q e -> q g e")
-            nc.sync.dma_start(out=rows, in_=res[1][:, :, c])
+        def gated(dst, y, g):
+            nc.vector.scalar_tensor_tensor(out=dst, in0=y, scalar=1.0 / 16.0, in1=g, op0=ALU.mult, op1=ALU.mult)
 
-        def values_head(g, b):
-            for c in range(CHUNKS):
-                values(0, c, g, y_banks[b][:, c])
+        def finish_chunk(i, b):
+            gated(res[i][:], y_banks[b][:].rearrange("p (h f) -> p h f", h=H), gate[i][:])
+            nc.sync.dma_start(out=dealt(out, i), in_=res[i][:])
 
-        def finish_head(g, b):
-            finish(0, slice(g, g + 1), 0, CHUNKS, y_banks[b][:].rearrange("p (g c) e -> p g (c e)", g=1))
-            store_head(0, g, 0, CHUNKS)
+        def finish_pair(a, i, b):
+            heads = HEAD_SLICE[a]
+            gated(res[i][:, heads], y_banks[b][:].rearrange("p (g f) -> p g f", g=2), gate[i][:, heads])
+            nc.sync.dma_start(out=dealt(out, i)[:, heads], in_=res[i][:, heads])
 
-        def values_outer(c0, c1, b):
-            for g in range(2):
-                for c in range(c0, c1):
-                    values(1, c, g, y_banks[b][:, g * (c1 - c0) + c - c0])
-
-        def finish_outer(c0, c1, b):
-            y = y_banks[b][:, : 2 * (c1 - c0)].rearrange("p (g c) e -> p g (c e)", g=2)
-            finish(1, slice(0, 2), c0, c1, y)
-
-        def values_last(g, b):
-            values(1, CHUNKS - 1, g, y_banks[b][:, 0])
-
-        def finish_last(g, b):
-            finish(1, slice(g, g + 1), CHUNKS - 1, CHUNKS, y_banks[b][:, 0:1])
-            store_head(1, g, CHUNKS - 1, CHUNKS)
+        def finish_part(a, i, g, e0, e1, b):
+            h = HEADS[a][g]
+            part = slice(e0 * E, e1 * E)
+            first = g * width[i] * E
+            gated(res[i][:, h, part], y_banks[b][:, first + e0 * E : first + e1 * E], gate[i][:, h, part])
+            nc.sync.dma_start(out=dealt(out, i)[:, h, part], in_=res[i][:, h, part])
 
         def cast_v():
             nc.scalar.copy(
@@ -230,110 +240,118 @@ def tile_rows_a_relu_mask_gate_kernel(tc, qT, kT, t, v, mask, og, out):
                 out=v_codes[:].bitcast(FP8X4), scales=v_scales[:], in_=v_bf[:].rearrange("p g e j -> p (g e j)")
             )
 
-        def load_v():
-            nc.sync.dma_start(
-                out=v_raw[:].rearrange("p g j e -> p g (j e)"), in_=v.rearrange("g (p j) e -> p g (j e)", j=PACK)
-            )
-
         def keys():
             k_src = k_raw[:].rearrange("p j (s r) -> p s r j", r=PACK)
             k_dst = k_bf[:].rearrange("p r s j -> p s r j")
             nc.vector.tensor_copy(out=k_dst[:, :K_SPLIT], in_=k_src[:, :K_SPLIT])
             nc.scalar.copy(out=k_dst[:, K_SPLIT:], in_=k_src[:, K_SPLIT:])
+
+        def quant_k(u):
+            part = slice(2 * u * P, 2 * (u + 1) * P)
             nc.vector.quantize_mx(
-                out=k_codes[:].bitcast(FP8X4), scales=k_scales[:], in_=k_bf[:].rearrange("p r s j -> p (r s j)")
+                out=k_codes[:, part].bitcast(FP8X4),
+                scales=k_scales[:, part],
+                in_=k_bf[:, 2 * u : 2 * u + 2].rearrange("p r s j -> p (r s j)"),
             )
 
+        every = slice(0, H)
+        on_s = nc.scalar.copy
+        on_v = nc.vector.tensor_copy
         nc.sync.dma_start(out=k_raw[:], in_=kT.rearrange("g (p j) n -> (g p) j n", j=PACK))
-        nc.scalar.dma_start(out=t_sb[:], in_=t.rearrange("(s r) o -> s (r o)", r=PACK))
-        load_q_adjacent(0)
+        nc.sync.dma_start(out=t_sb[:], in_=t.rearrange("(s r) o -> s (r o)", r=PACK))
+        load_q_first()
         load_mask(0)
-        load_q_adjacent(1)
-        load_mask(1)
-        load_q_outer(0, 0, nc.sync)
-        load_q_outer(1, 0, nc.sync)
+        load_q(1, 0)
+        load_q(1, 1)
         nc.vector.memset(warm[:, 0:1], 0.0)
         nc.scalar.activation(out=warm[:, 1:2], in_=warm[:, 0:1], func=ACT.Sigmoid)
+        load_q(0, 2)
+        load_mask(1)
+        load_q(1, 2)
         load_v()
-        load_q_outer(0, 1, nc.sync)
-        load_q_outer(1, 1, nc.sync)
-        load_og(1)
-        load_og(2)
-        load_og(0)
-        load_og(3)
+        load_og(0, every)
+        load_og(1, every)
+        load_og(2, HEAD_SLICE[0])
+        load_og(2, HEAD_SLICE[1])
         keys()
-        cast_q(0, 0)
-        cast_q(0, 1)
-        quant_q(0, 0, 1)
-        scores_tile_by_tile(0, 0)
-        mt_vector(0)
-        quant_q(0, 1, 2)
-        scores_tile_by_tile(0, 1)
-        scale_mask(1)
-        weave_mask(1)
-        cast_q(0, 2)
-        cast_q(0, 3)
-        scale_mask(3)
-        weave_mask(3)
-        cast_q(1, 0)
-        cast_q(1, 1)
+        cast_q(0, 1, 0, on_s)
+        scale_mask(1, 0)
+        weave_mask(1, 0)
+        cast_q(1, 0, 0, on_s)
+        cast_q(1, 1, 0, on_s)
+        cast_q_both(0, 2)
+        scale_mask(2, 0)
+        scale_mask(2, 1)
+        weave_mask(2, 0)
+        weave_mask(2, 1)
+        cast_q(1, 2, 0, on_s)
+        cast_q(1, 2, 1, on_s)
         cast_v()
-        cast_q(1, 2)
-        cast_q(1, 3)
-        sigmoid(0, 0)
-        sigmoid(0, 1)
-        sigmoid(1, 0)
-        sigmoid(1, 1)
-        weigh(0, 0, 0)
-        weigh(0, 0, 1)
-        weigh(0, 1, 0)
-        quant_q(0, 2, 3)
-        scores_tile_by_tile(0, 2)
-        weigh(0, 1, 1)
-        quant_q(0, 3, 4)
-        scores_tile_by_tile(0, 3)
-        mt_vector(2)
-        quant_w(0, 0, 0, 4)
-        weigh(0, 2, 0)
-        weigh(0, 2, 1)
-        weigh(0, 3, 0)
-        quant_q(1, 0, 1)
-        scores_tile_by_tile(1, 0)
-        weigh(0, 3, 1)
-        quant_q(1, 1, 2)
-        scores_tile_by_tile(1, 1)
-        quant_w(0, 1, 0, 4)
-        quant_v()
-        values_head(0, 0)
-        values_head(1, 1)
-        weigh(1, 0, 0)
-        weigh(1, 0, 1)
-        weigh(1, 1, 0)
-        quant_q(1, 2, 3)
-        scores_tile_by_tile(1, 2)
-        weigh(1, 1, 1)
-        quant_q(1, 3, 4)
-        scores_tile_by_tile(1, 3)
-        finish_head(0, 0)
-        quant_w(1, 0, 0, 4)
-        values_outer(0, 1, 0)
-        finish_head(1, 1)
-        values_outer(1, 2, 1)
-        weigh(1, 2, 0)
-        weigh(1, 2, 1)
-        weigh(1, 3, 0)
-        finish_outer(0, 1, 0)
-        store_outer_chunk(0)
+        sigmoid(0, every)
+        sigmoid(1, every)
+        sigmoid(2, HEAD_SLICE[0])
+        sigmoid(2, HEAD_SLICE[1])
+        quant_k(0)
+        cast_q(0, 0, 0, on_v)
+        quant_k(1)
+        quant_q(0, 0, 0, 1)
+        scores(0, 0, 0, 0)
+        scores(0, 0, 0, 1)
+        quant_q(0, 1, 0, 1)
+        scores(0, 1, 0, 0)
+        scores(0, 1, 0, 1)
+        mt_vector(0, 0)
+        weigh(0, 0, 0, 0)
+        weigh(0, 0, 0, 1)
+        weigh(0, 1, 0, 0)
+        quant_q(1, 0, 0, 1)
+        scores(1, 0, 0, 0)
+        scores(1, 0, 0, 1)
+        weigh(0, 1, 0, 1)
+        quant_w(0, 0, 0, 2)
+        quant_q(1, 1, 0, 1)
+        scores(1, 1, 0, 0)
+        scores(1, 1, 0, 1)
+        weigh(1, 0, 0, 0)
+        quant_w(0, 1, 0, 2)
+        weigh(1, 0, 0, 1)
+        weigh(1, 1, 0, 0)
+        quant_q(0, 2, 0, 2)
+        scores(0, 2, 0, 0)
+        scores(0, 2, 0, 1)
+        scores(0, 2, 1, 0)
+        weigh(1, 1, 0, 1)
+        scores(0, 2, 1, 1)
+        quant_w(1, 0, 0, 2)
         quant_w(1, 1, 0, 2)
-        values_outer(2, 3, 0)
-        weigh(1, 3, 1)
-        quant_w(1, 1, 2, 3)
-        finish_outer(2, 3, 0)
-        store_outer_chunk(2)
-        values_last(0, 0)
-        quant_w(1, 1, 3, 4)
-        finish_outer(1, 2, 1)
-        store_outer_chunk(1)
-        values_last(1, 1)
-        finish_last(0, 0)
-        finish_last(1, 1)
+        weigh(0, 2, 0, 0)
+        weigh(0, 2, 0, 1)
+        quant_q(1, 2, 0, 1)
+        scores(1, 2, 0, 0)
+        scores(1, 2, 0, 1)
+        weigh(0, 2, 1, 0)
+        quant_q(1, 2, 1, 2)
+        scores(1, 2, 1, 0)
+        scores(1, 2, 1, 1)
+        weigh(0, 2, 1, 1)
+        weigh(1, 2, 0, 0)
+        quant_v()
+        values_chunk(0, 0)
+        values_chunk(1, 1)
+        quant_w(0, 2, 0, 4)
+        weigh(1, 2, 1, 0)
+        finish_chunk(0, 0)
+        values(0, 2, 0, 4, 0)
+        quant_w(1, 2, 0, 2)
+        finish_chunk(1, 1)
+        values(1, 2, 0, 2, 1)
+        weigh(1, 2, 0, 1)
+        finish_pair(0, 2, 0)
+        quant_w(1, 2, 2, 3)
+        values(1, 2, 2, 3, 0)
+        weigh(1, 2, 1, 1)
+        finish_part(1, 2, 0, 0, 2, 1)
+        quant_w(1, 2, 3, 4)
+        values(1, 2, 3, 4, 1)
+        finish_part(1, 2, 1, 0, 1, 0)
+        finish_part(1, 2, 1, 1, 2, 1)

@@ -18,7 +18,7 @@ ROWS = 64
 PACK = 4
 QC = 128
 K_SPLIT = 84
-SCORE_BANKS = 3
+SCORE_BANKS = (3, 2)
 HEADS = ((1, 2), (0, 3))
 HEAD_SLICE = (slice(1, 3), slice(0, 4, 3))
 PIECES = ((0, 1), (128, 1), (256, 2))
@@ -63,9 +63,9 @@ def tile_rows_a_relu_mask_gate_kernel(tc, qT, kT, t, v, mask, og, out):
         m_scaled = {(i, e): tile("m_scaled%d%d" % (i, e), [P, PACK, QC], F32) for i in (1, 2) for e in range(width[i])}
         mt = {(i, e): tile("mt%d%d" % (i, e), [P, QC, PACK], F32) for i in range(3) for e in range(width[i])}
         score_banks = [
-            [ps.tile([P, PACK, QC], F32, name="score%d%d" % (g, b)) for b in range(SCORE_BANKS)] for g in range(2)
+            [ps.tile([P, PACK, QC], F32, name="score%d%d" % (g, b)) for b in range(SCORE_BANKS[g])] for g in range(2)
         ]
-        y_banks = [ps.tile([P, PACK * E], F32, name="y%d" % b) for b in range(2)]
+        y_banks = [ps.tile([P, PACK * E], F32, name="y%d" % b) for b in range(8 - sum(SCORE_BANKS))]
 
         def cols(c):
             return slice(c * QC, (c + 1) * QC)
@@ -126,16 +126,16 @@ def tile_rows_a_relu_mask_gate_kernel(tc, qT, kT, t, v, mask, og, out):
                 in_=q_bf[a, i][:, e0:e1].rearrange("p e q j -> p (e q j)"),
             )
 
-        def mt_vector(i, e):
+        def mt_vector(i, e, part):
             nc.vector.tensor_tensor(
-                out=mt[i, e][:].rearrange("p (c i) r -> p c r i", i=2),
-                in0=mask_of(i, e).rearrange("p r (c i) -> p c r i", i=2),
-                in1=t_sb[:, 0:PACK].unsqueeze(1).unsqueeze(3).to_broadcast([P, QC // 2, PACK, 2]),
+                out=mt[i, e][:, part].rearrange("p (c i) r -> p c r i", i=2),
+                in0=mask_of(i, e)[:, :, part].rearrange("p r (c i) -> p c r i", i=2),
+                in1=t_sb[:, 0:PACK].unsqueeze(1).unsqueeze(3).to_broadcast([P, (part.stop - part.start) // 2, PACK, 2]),
                 op=ALU.mult,
             )
 
-        def scale_mask(i, e):
-            for r in range(PACK):
+        def scale_mask(i, e, places=range(PACK)):
+            for r in places:
                 nc.scalar.activation(
                     out=m_scaled[i, e][:, r, :],
                     in_=mask_of(i, e)[:, r],
@@ -154,7 +154,7 @@ def tile_rows_a_relu_mask_gate_kernel(tc, qT, kT, t, v, mask, og, out):
 
         def scores(a, i, e, g):
             rows = slice(ROWS * g, ROWS * (g + 1))
-            bank = score_banks[g][turn[g] % SCORE_BANKS]
+            bank = score_banks[g][turn[g] % SCORE_BANKS[g]]
             turn[g] = turn[g] + 1
             held[a, i, e, g] = bank
             for r in range(PACK):
@@ -168,12 +168,12 @@ def tile_rows_a_relu_mask_gate_kernel(tc, qT, kT, t, v, mask, og, out):
                     stop=True,
                 )
 
-        def weigh(a, i, e, g):
+        def weigh(a, i, e, g, part=slice(0, QC)):
             nc.vector.scalar_tensor_tensor(
-                out=w_bf[a, i][:, g * width[i] + e],
-                in0=held[a, i, e, g][:].rearrange("p r q -> p q r"),
+                out=w_bf[a, i][:, g * width[i] + e, part],
+                in0=held[a, i, e, g][:, :, part].rearrange("p r q -> p q r"),
                 scalar=0.0,
-                in1=mt[i, e][:],
+                in1=mt[i, e][:, part],
                 op0=ALU.max,
                 op1=ALU.mult,
             )
@@ -255,6 +255,7 @@ def tile_rows_a_relu_mask_gate_kernel(tc, qT, kT, t, v, mask, og, out):
             )
 
         every = slice(0, H)
+        low, high = slice(0, QC // 2), slice(QC // 2, QC)
         on_s = nc.scalar.copy
         on_v = nc.vector.tensor_copy
         nc.sync.dma_start(out=k_raw[:], in_=kT.rearrange("g (p j) n -> (g p) j n", j=PACK))
@@ -300,8 +301,10 @@ def tile_rows_a_relu_mask_gate_kernel(tc, qT, kT, t, v, mask, og, out):
         quant_q(0, 1, 0, 1)
         scores(0, 1, 0, 0)
         scores(0, 1, 0, 1)
-        mt_vector(0, 0)
-        weigh(0, 0, 0, 0)
+        mt_vector(0, 0, low)
+        mt_vector(0, 0, high)
+        weigh(0, 0, 0, 0, low)
+        weigh(0, 0, 0, 0, high)
         weigh(0, 0, 0, 1)
         weigh(0, 1, 0, 0)
         quant_q(1, 0, 0, 1)
@@ -332,26 +335,27 @@ def tile_rows_a_relu_mask_gate_kernel(tc, qT, kT, t, v, mask, og, out):
         weigh(0, 2, 1, 0)
         quant_q(1, 2, 1, 2)
         scores(1, 2, 1, 0)
-        scores(1, 2, 1, 1)
         weigh(0, 2, 1, 1)
+        scores(1, 2, 1, 1)
         weigh(1, 2, 0, 0)
         quant_v()
         values_chunk(0, 0)
         values_chunk(1, 1)
         quant_w(0, 2, 0, 4)
+        values(0, 2, 0, 4, 2)
         weigh(1, 2, 1, 0)
         finish_chunk(0, 0)
-        values(0, 2, 0, 4, 0)
         quant_w(1, 2, 0, 2)
+        values(1, 2, 0, 2, 0)
         finish_chunk(1, 1)
-        values(1, 2, 0, 2, 1)
         weigh(1, 2, 0, 1)
-        finish_pair(0, 2, 0)
+        finish_part(0, 2, 0, 0, 2, 2)
         quant_w(1, 2, 2, 3)
-        values(1, 2, 2, 3, 0)
+        values(1, 2, 2, 3, 1)
         weigh(1, 2, 1, 1)
-        finish_part(1, 2, 0, 0, 2, 1)
+        finish_part(1, 2, 0, 0, 2, 0)
         quant_w(1, 2, 3, 4)
-        values(1, 2, 3, 4, 1)
-        finish_part(1, 2, 1, 0, 1, 0)
-        finish_part(1, 2, 1, 1, 2, 1)
+        values(1, 2, 3, 4, 0)
+        finish_part(0, 2, 1, 0, 2, 2)
+        finish_part(1, 2, 1, 0, 1, 1)
+        finish_part(1, 2, 1, 1, 2, 0)

@@ -20,8 +20,8 @@ QC = 128
 K_SPLIT = 84
 SCORE_BANKS = (3, 2)
 HEADS = ((1, 2), (0, 3))
-HEAD_SLICE = (slice(1, 3), slice(0, 4, 3))
-PIECES = ((0, 1), (128, 1), (256, 2))
+PAIR = (slice(1, 3), slice(0, 4, 3))
+MASK_PIECES = ((0, 2), (256, 2))
 
 
 def tile_rows_a_relu_mask_gate_kernel(tc, qT, kT, t, v, mask, og, out):
@@ -44,24 +44,22 @@ def tile_rows_a_relu_mask_gate_kernel(tc, qT, kT, t, v, mask, og, out):
         v_bf = tile("v_bf", [P, KV, E, PACK], BF16)
         v_codes = tile("v_codes", [P, KV * E], I32)
         v_scales = tile("v_scales", [P, KV * E], U8)
-        width = [n for q0, n in PIECES]
-        both = [(a, i) for a in range(2) for i in range(len(PIECES))]
-        q_raw = {x: tile("q_raw%d%d" % x, [P, PACK, width[x[1]] * QC], F32) for x in both if x > (0, 1)}
-        q_first = tile("q_first", [P, PACK, 2 * QC], F32)
-        q_raw[0, 0] = q_first[:, :, :QC]
-        q_raw[0, 1] = q_first[:, :, QC:]
-        q_bf = {x: tile("q_bf%d%d" % x, [P, width[x[1]], QC, PACK], BF16) for x in both}
-        q_codes = {x: tile("q_codes%d%d" % x, [P, width[x[1]] * QC], I32) for x in both}
-        q_scales = {x: tile("q_scales%d%d" % x, [P, width[x[1]] * QC], U8) for x in both}
-        w_bf = {x: tile("w_bf%d%d" % x, [P, 2 * width[x[1]], QC, PACK], BF16) for x in both}
-        w_codes = {x: tile("w_codes%d%d" % x, [P, 2 * width[x[1]] * QC], I32) for x in both}
-        w_scales = {x: tile("w_scales%d%d" % x, [P, 2 * width[x[1]] * QC], U8) for x in both}
-        og_raw = [tile("og_raw%d" % i, [P, H, n * E], F32) for i, n in enumerate(width)]
-        gate = [tile("gate%d" % i, [P, H, n * E], F32) for i, n in enumerate(width)]
-        res = [tile("res%d" % i, [P, H, n * E], F32) for i, n in enumerate(width)]
-        m_raw = [tile("m_raw%d" % u, [P, PACK, 2 * QC], F32) for u in range(2)]
-        m_scaled = {(i, e): tile("m_scaled%d%d" % (i, e), [P, PACK, QC], F32) for i in (1, 2) for e in range(width[i])}
-        mt = {(i, e): tile("mt%d%d" % (i, e), [P, QC, PACK], F32) for i in range(3) for e in range(width[i])}
+        halves = [(a, u) for a in range(2) for u in range(2)]
+        q_half = {x: tile("q_half%d%d" % x, [P, PACK, 2 * QC], F32) for x in halves if x != (1, 0)}
+        q_piece = [tile("q_piece%d" % e, [P, PACK, QC], F32) for e in range(2)]
+        q_bf = {x: tile("q_bf%d%d" % x, [P, 2, QC, PACK], BF16) for x in halves}
+        q_codes = {x: tile("q_codes%d%d" % x, [P, 2 * QC], I32) for x in halves}
+        q_scales = {x: tile("q_scales%d%d" % x, [P, 2 * QC], U8) for x in halves}
+        w_bf = {x: tile("w_bf%d%d" % x, [P, 4, QC, PACK], BF16) for x in halves}
+        w_codes = {x: tile("w_codes%d%d" % x, [P, 4 * QC], I32) for x in halves}
+        w_scales = {x: tile("w_scales%d%d" % x, [P, 4 * QC], U8) for x in halves}
+        og_raw = [tile("og_raw%d" % i, [P, H, n * E], F32) for i, n in enumerate((1, 1, 2))]
+        gate = [tile("gate%d" % i, [P, H, n * E], F32) for i, n in enumerate((1, 1, 2))]
+        res = [tile("res%d" % i, [P, H, n * E], F32) for i, n in enumerate((1, 1, 2))]
+        m_raw = [tile("m_raw%d" % i, [P, PACK, n * QC], F32) for i, (q0, n) in enumerate(MASK_PIECES)]
+        m_scaled = [tile("m_scaled%d" % u, [P, PACK, (u + 1) * QC], F32) for u in range(2)]
+        mt = {x: tile("mt%d%d" % x, [P, QC, PACK], F32) for x in halves}
+        relu_sb = tile("relu_sb", [P, QC, PACK], F32)
         score_banks = [
             [ps.tile([P, PACK, QC], F32, name="score%d%d" % (g, b)) for b in range(SCORE_BANKS[g])] for g in range(2)
         ]
@@ -70,142 +68,163 @@ def tile_rows_a_relu_mask_gate_kernel(tc, qT, kT, t, v, mask, og, out):
         def cols(c):
             return slice(c * QC, (c + 1) * QC)
 
-        def span(i):
-            return slice(PIECES[i][0], PIECES[i][0] + width[i] * QC)
+        def half_cols(u):
+            return slice(2 * u * QC, 2 * (u + 1) * QC)
 
-        def load_q(a, i):
-            if a == 0:
-                rows = qT[1:3].rearrange("g (p j) q -> (g p) j q", j=PACK)
-                nc.sync.dma_start(out=q_raw[a, i][:], in_=rows[:, :, span(i)])
-            else:
-                for g in range(2):
-                    rows = qT[HEADS[a][g]].rearrange("(p j) q -> p j q", j=PACK)
-                    nc.sync.dma_start(out=q_raw[a, i][ROWS * g : ROWS * (g + 1)], in_=rows[:, :, span(i)])
-
-        def load_q_first():
+        def load_q_inner(u):
             rows = qT[1:3].rearrange("g (p j) q -> (g p) j q", j=PACK)
-            nc.sync.dma_start(out=q_first[:], in_=rows[:, :, : 2 * QC])
+            nc.sync.dma_start(out=q_half[0, u][:], in_=rows[:, :, half_cols(u)])
 
-        def load_mask(u):
+        def load_q_outer(dst, part):
+            for g in range(2):
+                rows = qT[HEADS[1][g]].rearrange("(p j) q -> p j q", j=PACK)
+                nc.sync.dma_start(out=dst[ROWS * g : ROWS * (g + 1)], in_=rows[:, :, part])
+
+        def load_mask(i):
+            q0, n = MASK_PIECES[i]
             rows = mask.rearrange("(s r) q -> s r q", r=PACK)
-            nc.sync.dma_start(out=m_raw[u][:], in_=rows[:, :, 2 * u * QC : 2 * (u + 1) * QC])
+            nc.sync.dma_start(out=m_raw[i][:], in_=rows[:, :, q0 : q0 + n * QC])
 
-        def mask_of(i, e):
-            u, first = divmod(PIECES[i][0], 2 * QC)
-            return m_raw[u][:, :, first + e : first + width[i] * QC : width[i]]
+        def first_mask(e):
+            i = max(x for x, (q0, n) in enumerate(MASK_PIECES) if q0 <= e * QC)
+            return m_raw[i][:, :, e * QC - MASK_PIECES[i][0] : (e + 1) * QC - MASK_PIECES[i][0]]
 
-        def dealt(x, i):
-            return x[:, span(i)].rearrange("h (m e) f -> m h (e f)", m=QC)
+        def rows_of(x, i):
+            part = cols(i) if i < 2 else half_cols(1)
+            return x[:, part].rearrange("h (m e) f -> m h (e f)", m=QC)
 
         def load_og(i, heads):
-            nc.sync.dma_start(out=og_raw[i][:, heads], in_=dealt(og, i)[:, heads])
+            nc.sync.dma_start(out=og_raw[i][:, heads], in_=rows_of(og, i)[:, heads])
 
         def load_v():
             nc.sync.dma_start(
                 out=v_raw[:].rearrange("p g j e -> p g (j e)"), in_=v.rearrange("g (p j) e -> p g (j e)", j=PACK)
             )
 
-        def cast_q(a, i, e, copy):
-            n = width[i]
+        def cast_first(a, e, copy):
+            raw = q_piece[e][:] if a == 1 else q_half[0, 0][:, :, cols(e)]
             copy(
-                out=q_bf[a, i][:, e].rearrange("p (c i) j -> p c j i", i=4 // n),
-                in_=q_raw[a, i][:, :, e::n].rearrange("p j (c i) -> p c j i", i=4 // n),
+                out=q_bf[a, 0][:, e].rearrange("p (c i) j -> p c j i", i=4),
+                in_=raw.rearrange("p j (c i) -> p c j i", i=4),
             )
 
-        def cast_q_both(a, i):
+        def cast_dealt(a, e):
             nc.scalar.copy(
-                out=q_bf[a, i][:].rearrange("p e (c i) j -> p c j i e", i=2),
-                in_=q_raw[a, i][:].rearrange("p j (c i e) -> p c j i e", i=2, e=2),
+                out=q_bf[a, 1][:, e].rearrange("p (c i) j -> p c j i", i=2),
+                in_=q_half[a, 1][:, :, e::2].rearrange("p j (c i) -> p c j i", i=2),
             )
 
-        def quant_q(a, i, e0, e1):
+        def cast_dealt_both(a):
+            nc.scalar.copy(
+                out=q_bf[a, 1][:].rearrange("p e (c i) j -> p c j i e", i=2),
+                in_=q_half[a, 1][:].rearrange("p j (c i e) -> p c j i e", i=2, e=2),
+            )
+
+        def quant_q(a, u, e0, e1):
             part = slice(e0 * QC, e1 * QC)
             nc.vector.quantize_mx(
-                out=q_codes[a, i][:, part].bitcast(FP8X4),
-                scales=q_scales[a, i][:, part],
-                in_=q_bf[a, i][:, e0:e1].rearrange("p e q j -> p (e q j)"),
+                out=q_codes[a, u][:, part].bitcast(FP8X4),
+                scales=q_scales[a, u][:, part],
+                in_=q_bf[a, u][:, e0:e1].rearrange("p e q j -> p (e q j)"),
             )
 
-        def mt_vector(i, e, part):
+        def mt_vector(e, part):
             nc.vector.tensor_tensor(
-                out=mt[i, e][:, part].rearrange("p (c i) r -> p c r i", i=2),
-                in0=mask_of(i, e)[:, :, part].rearrange("p r (c i) -> p c r i", i=2),
+                out=mt[0, e][:, part].rearrange("p (c i) r -> p c r i", i=2),
+                in0=first_mask(e)[:, :, part].rearrange("p r (c i) -> p c r i", i=2),
                 in1=t_sb[:, 0:PACK].unsqueeze(1).unsqueeze(3).to_broadcast([P, (part.stop - part.start) // 2, PACK, 2]),
                 op=ALU.mult,
             )
 
-        def scale_mask(i, e, places=range(PACK)):
-            for r in places:
-                nc.scalar.activation(
-                    out=m_scaled[i, e][:, r, :],
-                    in_=mask_of(i, e)[:, r],
-                    func=ACT.Copy,
-                    scale=t_sb[:, r : r + 1],
-                )
+        def scale_mask(src, dst):
+            for r in range(PACK):
+                nc.scalar.activation(out=dst[:, r], in_=src[:, r], func=ACT.Copy, scale=t_sb[:, r : r + 1])
 
-        def weave_mask(i, e):
+        def scale_first():
+            scale_mask(first_mask(1), m_scaled[0][:])
+
+        def scale_dealt(e):
+            scale_mask(m_raw[-1][:, :, e::2], m_scaled[1][:, :, cols(e)])
+
+        def weave_mask(u, e):
+            src = m_scaled[0][:] if u == 0 else m_scaled[1][:, :, cols(e)]
             nc.scalar.copy(
-                out=mt[i, e][:].rearrange("p (c i) r -> p c r i", i=2),
-                in_=m_scaled[i, e][:].rearrange("p r (c i) -> p c r i", i=2),
+                out=mt[u, e][:].rearrange("p (c i) r -> p c r i", i=2), in_=src.rearrange("p r (c i) -> p c r i", i=2)
             )
 
         turn = [0, 0]
         held = {}
 
-        def scores(a, i, e, g):
+        def scores(a, u, e, g):
             rows = slice(ROWS * g, ROWS * (g + 1))
             bank = score_banks[g][turn[g] % SCORE_BANKS[g]]
             turn[g] = turn[g] + 1
-            held[a, i, e, g] = bank
+            held[a, u, e, g] = bank
             for r in range(PACK):
                 nc.tensor.matmul_mx(
                     out=bank[:, r, :],
                     lhsT=k_codes[rows, r * P : (r + 1) * P].bitcast(FP8X4),
                     lhsT_scale=k_scales[rows, r * P : (r + 1) * P],
-                    rhs=q_codes[a, i][rows, cols(e)].bitcast(FP8X4),
-                    rhs_scale=q_scales[a, i][rows, cols(e)],
+                    rhs=q_codes[a, u][rows, cols(e)].bitcast(FP8X4),
+                    rhs_scale=q_scales[a, u][rows, cols(e)],
                     start=True,
                     stop=True,
                 )
 
-        def weigh(a, i, e, g, part=slice(0, QC)):
+        def slot(u, e, g):
+            return 2 * e + g if u == 0 else 2 * g + e
+
+        def weigh(a, u, e, g, part=slice(0, QC)):
             nc.vector.scalar_tensor_tensor(
-                out=w_bf[a, i][:, g * width[i] + e, part],
-                in0=held[a, i, e, g][:, :, part].rearrange("p r q -> p q r"),
+                out=w_bf[a, u][:, slot(u, e, g), part],
+                in0=held[a, u, e, g][:, :, part].rearrange("p r q -> p q r"),
                 scalar=0.0,
-                in1=mt[i, e][:, part],
+                in1=mt[u, e][:, part],
                 op0=ALU.max,
                 op1=ALU.mult,
             )
 
-        def quant_w(a, i, s0, s1):
-            part = slice(s0 * QC, s1 * QC)
+        def empty_bank(a, u, e, g):
+            nc.scalar.activation(out=relu_sb[:], in_=held[a, u, e, g][:].rearrange("p r q -> p q r"), func=ACT.Relu)
+
+        def weigh_pool(u, e):
+            nc.gpsimd.tensor_tensor(out=w_bf[0, 1][:, 0], in0=relu_sb[:], in1=mt[u, e][:], op=ALU.mult)
+
+        def quant_pool():
             nc.vector.quantize_mx(
-                out=w_codes[a, i][:, part].bitcast(FP8X4),
-                scales=w_scales[a, i][:, part],
-                in_=w_bf[a, i][:, s0:s1].rearrange("p s q r -> p (s q r)"),
+                out=w_codes[1, 1][:, cols(2)].bitcast(FP8X4),
+                scales=w_scales[1, 1][:, cols(2)],
+                in_=w_bf[0, 1][:, 0].rearrange("p q r -> p (q r)"),
             )
 
-        def value_pass(a, i, s, y):
-            g = s // width[i]
+        def quant_w(a, u, s0, s1):
+            part = slice(s0 * QC, s1 * QC)
+            nc.vector.quantize_mx(
+                out=w_codes[a, u][:, part].bitcast(FP8X4),
+                scales=w_scales[a, u][:, part],
+                in_=w_bf[a, u][:, s0:s1].rearrange("p s q r -> p (s q r)"),
+            )
+
+        def value_pass(a, u, e, g, y):
+            s = slot(u, e, g)
             nc.tensor.matmul_mx(
                 out=y,
-                lhsT=w_codes[a, i][:, cols(s)].bitcast(FP8X4),
-                lhsT_scale=w_scales[a, i][:, cols(s)],
+                lhsT=w_codes[a, u][:, cols(s)].bitcast(FP8X4),
+                lhsT_scale=w_scales[a, u][:, cols(s)],
                 rhs=v_codes[:, cols(g)].bitcast(FP8X4),
                 rhs_scale=v_scales[:, cols(g)],
                 start=True,
                 stop=True,
             )
 
-        def values_chunk(i, b):
+        def values_chunk(e, b):
             for a in range(2):
                 for g in range(2):
-                    value_pass(a, i, g, y_banks[b][:, cols(HEADS[a][g])])
+                    value_pass(a, 0, e, g, y_banks[b][:, cols(HEADS[a][g])])
 
-        def values(a, i, s0, s1, b):
+        def values(a, s0, s1, b):
             for s in range(s0, s1):
-                value_pass(a, i, s, y_banks[b][:, cols(s)])
+                value_pass(a, 1, s % 2, s // 2, y_banks[b][:, cols(s)])
 
         def sigmoid(i, heads):
             nc.scalar.activation(out=gate[i][:, heads], in_=og_raw[i][:, heads], func=ACT.Sigmoid)
@@ -213,21 +232,19 @@ def tile_rows_a_relu_mask_gate_kernel(tc, qT, kT, t, v, mask, og, out):
         def gated(dst, y, g):
             nc.vector.scalar_tensor_tensor(out=dst, in0=y, scalar=1.0 / 16.0, in1=g, op0=ALU.mult, op1=ALU.mult)
 
-        def finish_chunk(i, b):
-            gated(res[i][:], y_banks[b][:].rearrange("p (h f) -> p h f", h=H), gate[i][:])
-            nc.sync.dma_start(out=dealt(out, i), in_=res[i][:])
+        def finish_chunk(e, b):
+            gated(res[e][:], y_banks[b][:].rearrange("p (h f) -> p h f", h=H), gate[e][:])
+            nc.sync.dma_start(out=rows_of(out, e), in_=res[e][:])
 
-        def finish_pair(a, i, b):
-            heads = HEAD_SLICE[a]
-            gated(res[i][:, heads], y_banks[b][:].rearrange("p (g f) -> p g f", g=2), gate[i][:, heads])
-            nc.sync.dma_start(out=dealt(out, i)[:, heads], in_=res[i][:, heads])
+        def finish_pair(a, b):
+            gated(res[2][:, PAIR[a]], y_banks[b][:].rearrange("p (g f) -> p g f", g=2), gate[2][:, PAIR[a]])
+            nc.sync.dma_start(out=rows_of(out, 2)[:, PAIR[a]], in_=res[2][:, PAIR[a]])
 
-        def finish_part(a, i, g, e0, e1, b):
+        def finish_part(a, g, e0, e1, b):
             h = HEADS[a][g]
             part = slice(e0 * E, e1 * E)
-            first = g * width[i] * E
-            gated(res[i][:, h, part], y_banks[b][:, first + e0 * E : first + e1 * E], gate[i][:, h, part])
-            nc.sync.dma_start(out=dealt(out, i)[:, h, part], in_=res[i][:, h, part])
+            gated(res[2][:, h, part], y_banks[b][:, (2 * g + e0) * E : (2 * g + e1) * E], gate[2][:, h, part])
+            nc.sync.dma_start(out=rows_of(out, 2)[:, h, part], in_=res[2][:, h, part])
 
         def cast_v():
             nc.scalar.copy(
@@ -240,122 +257,120 @@ def tile_rows_a_relu_mask_gate_kernel(tc, qT, kT, t, v, mask, og, out):
                 out=v_codes[:].bitcast(FP8X4), scales=v_scales[:], in_=v_bf[:].rearrange("p g e j -> p (g e j)")
             )
 
-        def keys():
+        def cast_keys():
             k_src = k_raw[:].rearrange("p j (s r) -> p s r j", r=PACK)
             k_dst = k_bf[:].rearrange("p r s j -> p s r j")
             nc.vector.tensor_copy(out=k_dst[:, :K_SPLIT], in_=k_src[:, :K_SPLIT])
             nc.scalar.copy(out=k_dst[:, K_SPLIT:], in_=k_src[:, K_SPLIT:])
 
-        def quant_k(u):
-            part = slice(2 * u * P, 2 * (u + 1) * P)
+        def quant_k(r0, r1):
             nc.vector.quantize_mx(
-                out=k_codes[:, part].bitcast(FP8X4),
-                scales=k_scales[:, part],
-                in_=k_bf[:, 2 * u : 2 * u + 2].rearrange("p r s j -> p (r s j)"),
+                out=k_codes[:, r0 * P : r1 * P].bitcast(FP8X4),
+                scales=k_scales[:, r0 * P : r1 * P],
+                in_=k_bf[:, r0:r1].rearrange("p r s j -> p (r s j)"),
             )
 
         every = slice(0, H)
         low, high = slice(0, QC // 2), slice(QC // 2, QC)
-        on_s = nc.scalar.copy
-        on_v = nc.vector.tensor_copy
         nc.sync.dma_start(out=k_raw[:], in_=kT.rearrange("g (p j) n -> (g p) j n", j=PACK))
         nc.sync.dma_start(out=t_sb[:], in_=t.rearrange("(s r) o -> s (r o)", r=PACK))
-        load_q_first()
+        load_q_inner(0)
         load_mask(0)
-        load_q(1, 0)
-        load_q(1, 1)
+        load_q_outer(q_piece[0], cols(0))
+        load_q_outer(q_piece[1], cols(1))
         nc.vector.memset(warm[:, 0:1], 0.0)
         nc.scalar.activation(out=warm[:, 1:2], in_=warm[:, 0:1], func=ACT.Sigmoid)
-        load_q(0, 2)
+        load_q_inner(1)
         load_mask(1)
-        load_q(1, 2)
+        load_q_outer(q_half[1, 1], half_cols(1))
         load_v()
         load_og(0, every)
         load_og(1, every)
-        load_og(2, HEAD_SLICE[0])
-        load_og(2, HEAD_SLICE[1])
-        keys()
-        cast_q(0, 1, 0, on_s)
-        scale_mask(1, 0)
+        load_og(2, PAIR[0])
+        load_og(2, PAIR[1])
+        cast_keys()
+        quant_k(0, 2)
+        cast_first(0, 0, nc.vector.tensor_copy)
+        cast_first(0, 1, nc.scalar.copy)
+        quant_k(2, 4)
+        scale_first()
+        weave_mask(0, 1)
+        cast_first(1, 0, nc.scalar.copy)
+        cast_first(1, 1, nc.scalar.copy)
+        cast_dealt_both(0)
+        scale_dealt(0)
+        scale_dealt(1)
         weave_mask(1, 0)
-        cast_q(1, 0, 0, on_s)
-        cast_q(1, 1, 0, on_s)
-        cast_q_both(0, 2)
-        scale_mask(2, 0)
-        scale_mask(2, 1)
-        weave_mask(2, 0)
-        weave_mask(2, 1)
-        cast_q(1, 2, 0, on_s)
-        cast_q(1, 2, 1, on_s)
+        weave_mask(1, 1)
+        cast_dealt(1, 0)
+        cast_dealt(1, 1)
         cast_v()
-        sigmoid(0, every)
-        sigmoid(1, every)
-        sigmoid(2, HEAD_SLICE[0])
-        sigmoid(2, HEAD_SLICE[1])
-        quant_k(0)
-        cast_q(0, 0, 0, on_v)
-        quant_k(1)
         quant_q(0, 0, 0, 1)
         scores(0, 0, 0, 0)
         scores(0, 0, 0, 1)
-        quant_q(0, 1, 0, 1)
-        scores(0, 1, 0, 0)
-        scores(0, 1, 0, 1)
-        mt_vector(0, 0, low)
-        mt_vector(0, 0, high)
+        quant_q(0, 0, 1, 2)
+        scores(0, 0, 1, 0)
+        scores(0, 0, 1, 1)
+        mt_vector(0, low)
+        mt_vector(0, high)
         weigh(0, 0, 0, 0, low)
         weigh(0, 0, 0, 0, high)
         weigh(0, 0, 0, 1)
-        weigh(0, 1, 0, 0)
+        weigh(0, 0, 1, 0)
         quant_q(1, 0, 0, 1)
         scores(1, 0, 0, 0)
         scores(1, 0, 0, 1)
-        weigh(0, 1, 0, 1)
+        weigh(0, 0, 1, 1)
         quant_w(0, 0, 0, 2)
+        quant_q(1, 0, 1, 2)
+        scores(1, 0, 1, 0)
+        scores(1, 0, 1, 1)
+        weigh(1, 0, 0, 0)
+        quant_w(0, 0, 2, 4)
+        weigh(1, 0, 0, 1)
+        weigh(1, 0, 1, 0)
+        quant_q(0, 1, 0, 2)
+        scores(0, 1, 0, 0)
+        scores(0, 1, 0, 1)
+        scores(0, 1, 1, 0)
+        weigh(1, 0, 1, 1)
+        scores(0, 1, 1, 1)
+        quant_w(1, 0, 0, 2)
+        quant_w(1, 0, 2, 4)
+        weigh(0, 1, 0, 0)
+        weigh(0, 1, 0, 1)
         quant_q(1, 1, 0, 1)
         scores(1, 1, 0, 0)
         scores(1, 1, 0, 1)
-        weigh(1, 0, 0, 0)
-        quant_w(0, 1, 0, 2)
-        weigh(1, 0, 0, 1)
+        sigmoid(0, every)
+        empty_bank(1, 1, 0, 1)
+        sigmoid(1, every)
+        sigmoid(2, PAIR[0])
+        sigmoid(2, PAIR[1])
+        weigh(0, 1, 1, 0)
+        quant_q(1, 1, 1, 2)
+        scores(1, 1, 1, 0)
+        weigh(0, 1, 1, 1)
+        scores(1, 1, 1, 1)
         weigh(1, 1, 0, 0)
-        quant_q(0, 2, 0, 2)
-        scores(0, 2, 0, 0)
-        scores(0, 2, 0, 1)
-        scores(0, 2, 1, 0)
-        weigh(1, 1, 0, 1)
-        scores(0, 2, 1, 1)
-        quant_w(1, 0, 0, 2)
-        quant_w(1, 1, 0, 2)
-        weigh(0, 2, 0, 0)
-        weigh(0, 2, 0, 1)
-        quant_q(1, 2, 0, 1)
-        scores(1, 2, 0, 0)
-        scores(1, 2, 0, 1)
-        weigh(0, 2, 1, 0)
-        quant_q(1, 2, 1, 2)
-        scores(1, 2, 1, 0)
-        weigh(0, 2, 1, 1)
-        scores(1, 2, 1, 1)
-        weigh(1, 2, 0, 0)
         quant_v()
         values_chunk(0, 0)
         values_chunk(1, 1)
-        quant_w(0, 2, 0, 4)
-        values(0, 2, 0, 4, 2)
-        weigh(1, 2, 1, 0)
+        quant_w(0, 1, 0, 4)
+        values(0, 0, 4, 2)
+        weigh_pool(1, 0)
+        weigh(1, 1, 1, 0)
         finish_chunk(0, 0)
-        quant_w(1, 2, 0, 2)
-        values(1, 2, 0, 2, 0)
         finish_chunk(1, 1)
-        weigh(1, 2, 0, 1)
-        finish_part(0, 2, 0, 0, 2, 2)
-        quant_w(1, 2, 2, 3)
-        values(1, 2, 2, 3, 1)
-        weigh(1, 2, 1, 1)
-        finish_part(1, 2, 0, 0, 2, 0)
-        quant_w(1, 2, 3, 4)
-        values(1, 2, 3, 4, 0)
-        finish_part(0, 2, 1, 0, 2, 2)
-        finish_part(1, 2, 1, 0, 1, 1)
-        finish_part(1, 2, 1, 1, 2, 0)
+        finish_part(0, 0, 0, 2, 2)
+        quant_w(1, 1, 0, 2)
+        quant_pool()
+        values(1, 0, 2, 0)
+        values(1, 2, 3, 1)
+        weigh(1, 1, 1, 1)
+        finish_part(0, 1, 0, 2, 2)
+        quant_w(1, 1, 3, 4)
+        values(1, 3, 4, 2)
+        finish_part(1, 0, 0, 2, 0)
+        finish_part(1, 1, 0, 1, 1)
+        finish_part(1, 1, 1, 2, 2)

@@ -258,8 +258,8 @@ def tile_rows_a_relu_mask_gate_kernel(tc, qT, kT, t, v, mask, og, out):
             )
 
         def cast_keys():
-            k_src = k_raw[:].rearrange("p j (s r) -> p s r j", r=PACK)
-            k_dst = k_bf[:].rearrange("p r s j -> p s r j")
+            k_src = k_raw[:].rearrange("p j (s r) -> p s j r", r=PACK)
+            k_dst = k_bf[:].rearrange("p r s j -> p s j r")
             nc.vector.tensor_copy(out=k_dst[:, :K_SPLIT], in_=k_src[:, :K_SPLIT])
             nc.scalar.copy(out=k_dst[:, K_SPLIT:], in_=k_src[:, K_SPLIT:])
 
@@ -273,7 +273,7 @@ def tile_rows_a_relu_mask_gate_kernel(tc, qT, kT, t, v, mask, og, out):
         every = slice(0, H)
         low, high = slice(0, QC // 2), slice(QC // 2, QC)
         nc.sync.dma_start(out=k_raw[:], in_=kT.rearrange("g (p j) n -> (g p) j n", j=PACK))
-        nc.sync.dma_start(out=t_sb[:], in_=t.rearrange("(s r) o -> s (r o)", r=PACK))
+        nc.scalar.dma_start(out=t_sb[:], in_=t.rearrange("(s r) o -> s (r o)", r=PACK))
         load_q_inner(0)
         load_mask(0)
         load_q_outer(q_piece[0], cols(0))

@@ -59,7 +59,7 @@ def tile_rows_a_relu_mask_gate_kernel(tc, qT, kT, t, v, mask, og, out):
         m_raw = [tile("m_raw%d" % i, [P, PACK, n * QC], F32) for i, (q0, n) in enumerate(MASK_PIECES)]
         m_scaled = [tile("m_scaled%d" % u, [P, PACK, (u + 1) * QC], F32) for u in range(2)]
         mt = {x: tile("mt%d%d" % x, [P, QC, PACK], F32) for x in halves}
-        relu_sb = tile("relu_sb", [P, QC, PACK], F32)
+        relu_sb = [tile("relu_sb%d" % e, [P, QC, PACK], F32) for e in range(2)]
         score_banks = [
             [ps.tile([P, PACK, QC], F32, name="score%d%d" % (g, b)) for b in range(SCORE_BANKS[g])] for g in range(2)
         ]
@@ -184,17 +184,32 @@ def tile_rows_a_relu_mask_gate_kernel(tc, qT, kT, t, v, mask, og, out):
                 op1=ALU.mult,
             )
 
-        def empty_bank(a, u, e, g):
-            nc.scalar.activation(out=relu_sb[:], in_=held[a, u, e, g][:].rearrange("p r q -> p q r"), func=ACT.Relu)
+        def empty_bank(e, part):
+            nc.scalar.activation(
+                out=relu_sb[e][:, part], in_=held[1, 1, e, 1][:, :, part].rearrange("p r q -> p q r"), func=ACT.Relu
+            )
 
-        def weigh_pool(u, e):
-            nc.gpsimd.tensor_tensor(out=w_bf[0, 1][:, 0], in0=relu_sb[:], in1=mt[u, e][:], op=ALU.mult)
+        def weigh_pool(e, part):
+            nc.gpsimd.tensor_tensor(
+                out=w_bf[0, 1][:, e, part], in0=relu_sb[e][:, part], in1=mt[1, e][:, part], op=ALU.mult
+            )
 
-        def quant_pool():
+        def weigh_rest(e, part):
+            nc.vector.scalar_tensor_tensor(
+                out=w_bf[0, 1][:, e, part],
+                in0=held[1, 1, e, 1][:, :, part].rearrange("p r q -> p q r"),
+                scalar=0.0,
+                in1=mt[1, e][:, part],
+                op0=ALU.max,
+                op1=ALU.mult,
+            )
+
+        def quant_pool(e0, e1):
+            part = slice((2 + e0) * QC, (2 + e1) * QC)
             nc.vector.quantize_mx(
-                out=w_codes[1, 1][:, cols(2)].bitcast(FP8X4),
-                scales=w_scales[1, 1][:, cols(2)],
-                in_=w_bf[0, 1][:, 0].rearrange("p q r -> p (q r)"),
+                out=w_codes[1, 1][:, part].bitcast(FP8X4),
+                scales=w_scales[1, 1][:, part],
+                in_=w_bf[0, 1][:, e0:e1].rearrange("p s q r -> p (s q r)"),
             )
 
         def quant_w(a, u, s0, s1):
@@ -271,7 +286,7 @@ def tile_rows_a_relu_mask_gate_kernel(tc, qT, kT, t, v, mask, og, out):
             )
 
         every = slice(0, H)
-        low, high = slice(0, QC // 2), slice(QC // 2, QC)
+        low, high, whole = slice(0, QC // 2), slice(QC // 2, QC), slice(0, QC)
         nc.sync.dma_start(out=k_raw[:], in_=kT.rearrange("g (p j) n -> (g p) j n", j=PACK))
         nc.scalar.dma_start(out=t_sb[:], in_=t.rearrange("(s r) o -> s (r o)", r=PACK))
         load_q_inner(0)
@@ -343,34 +358,33 @@ def tile_rows_a_relu_mask_gate_kernel(tc, qT, kT, t, v, mask, og, out):
         scores(1, 1, 0, 0)
         scores(1, 1, 0, 1)
         sigmoid(0, every)
-        empty_bank(1, 1, 0, 1)
+        empty_bank(0, whole)
         sigmoid(1, every)
-        sigmoid(2, PAIR[0])
-        sigmoid(2, PAIR[1])
         weigh(0, 1, 1, 0)
         quant_q(1, 1, 1, 2)
         scores(1, 1, 1, 0)
         weigh(0, 1, 1, 1)
         scores(1, 1, 1, 1)
-        weigh(1, 1, 0, 0)
+        empty_bank(1, low)
+        sigmoid(2, PAIR[0])
+        sigmoid(2, PAIR[1])
         quant_v()
         values_chunk(0, 0)
         values_chunk(1, 1)
         quant_w(0, 1, 0, 4)
         values(0, 0, 4, 2)
-        weigh_pool(1, 0)
+        weigh_pool(0, whole)
+        weigh_pool(1, low)
+        weigh(1, 1, 0, 0)
         weigh(1, 1, 1, 0)
+        weigh_rest(1, high)
         finish_chunk(0, 0)
         finish_chunk(1, 1)
         finish_part(0, 0, 0, 2, 2)
         quant_w(1, 1, 0, 2)
-        quant_pool()
         values(1, 0, 2, 0)
-        values(1, 2, 3, 1)
-        weigh(1, 1, 1, 1)
+        quant_pool(0, 2)
+        values(1, 2, 4, 1)
         finish_part(0, 1, 0, 2, 2)
-        quant_w(1, 1, 3, 4)
-        values(1, 3, 4, 2)
         finish_part(1, 0, 0, 2, 0)
-        finish_part(1, 1, 0, 1, 1)
-        finish_part(1, 1, 1, 2, 2)
+        finish_part(1, 1, 0, 2, 1)

@@ -155,21 +155,22 @@ def tile_rows_a_relu_mask_gate_kernel(tc, qT, kT, t, v, mask, og, out):
         turn = [0, 0]
         held = {}
 
-        def scores(a, u, e, g):
-            rows = slice(ROWS * g, ROWS * (g + 1))
-            bank = score_banks[g][turn[g] % SCORE_BANKS[g]]
-            turn[g] = turn[g] + 1
-            held[a, u, e, g] = bank
+        def scores(a, u, e, tiles):
+            for g in tiles:
+                held[a, u, e, g] = score_banks[g][turn[g] % SCORE_BANKS[g]]
+                turn[g] = turn[g] + 1
             for r in range(PACK):
-                nc.tensor.matmul_mx(
-                    out=bank[:, r, :],
-                    lhsT=k_codes[rows, r * P : (r + 1) * P].bitcast(FP8X4),
-                    lhsT_scale=k_scales[rows, r * P : (r + 1) * P],
-                    rhs=q_codes[a, u][rows, cols(e)].bitcast(FP8X4),
-                    rhs_scale=q_scales[a, u][rows, cols(e)],
-                    start=True,
-                    stop=True,
-                )
+                for g in tiles:
+                    rows = slice(ROWS * g, ROWS * (g + 1))
+                    nc.tensor.matmul_mx(
+                        out=held[a, u, e, g][:, r, :],
+                        lhsT=k_codes[rows, r * P : (r + 1) * P].bitcast(FP8X4),
+                        lhsT_scale=k_scales[rows, r * P : (r + 1) * P],
+                        rhs=q_codes[a, u][rows, cols(e)].bitcast(FP8X4),
+                        rhs_scale=q_scales[a, u][rows, cols(e)],
+                        start=True,
+                        stop=True,
+                    )
 
         def slot(u, e, g):
             return 2 * e + g if u == 0 else 2 * g + e
@@ -321,11 +322,11 @@ def tile_rows_a_relu_mask_gate_kernel(tc, qT, kT, t, v, mask, og, out):
         cast_dealt(1, 1)
         cast_v()
         quant_q(0, 0, 0, 1)
-        scores(0, 0, 0, 0)
-        scores(0, 0, 0, 1)
+        scores(0, 0, 0, (0,))
+        scores(0, 0, 0, (1,))
         quant_q(0, 0, 1, 2)
-        scores(0, 0, 1, 0)
-        scores(0, 0, 1, 1)
+        scores(0, 0, 1, (0,))
+        scores(0, 0, 1, (1,))
         mt_vector(0, low)
         mt_vector(0, high)
         weigh(0, 0, 0, 0, low)
@@ -333,38 +334,34 @@ def tile_rows_a_relu_mask_gate_kernel(tc, qT, kT, t, v, mask, og, out):
         weigh(0, 0, 0, 1)
         weigh(0, 0, 1, 0)
         quant_q(1, 0, 0, 1)
-        scores(1, 0, 0, 0)
-        scores(1, 0, 0, 1)
+        scores(1, 0, 0, (0,))
+        scores(1, 0, 0, (1,))
         weigh(0, 0, 1, 1)
         quant_w(0, 0, 0, 2)
         quant_q(1, 0, 1, 2)
-        scores(1, 0, 1, 0)
-        scores(1, 0, 1, 1)
+        scores(1, 0, 1, (0, 1))
         weigh(1, 0, 0, 0)
         quant_w(0, 0, 2, 4)
         weigh(1, 0, 0, 1)
-        weigh(1, 0, 1, 0)
         quant_q(0, 1, 0, 2)
-        scores(0, 1, 0, 0)
-        scores(0, 1, 0, 1)
-        scores(0, 1, 1, 0)
+        scores(0, 1, 0, (0, 1))
+        weigh(1, 0, 1, 0)
+        scores(0, 1, 1, (0,))
         weigh(1, 0, 1, 1)
-        scores(0, 1, 1, 1)
+        scores(0, 1, 1, (1,))
         quant_w(1, 0, 0, 2)
         quant_w(1, 0, 2, 4)
         weigh(0, 1, 0, 0)
         weigh(0, 1, 0, 1)
         quant_q(1, 1, 0, 1)
-        scores(1, 1, 0, 0)
-        scores(1, 1, 0, 1)
+        scores(1, 1, 0, (0, 1))
         sigmoid(0, every)
         empty_bank(0, whole)
         sigmoid(1, every)
-        weigh(0, 1, 1, 0)
-        quant_q(1, 1, 1, 2)
-        scores(1, 1, 1, 0)
         weigh(0, 1, 1, 1)
-        scores(1, 1, 1, 1)
+        quant_q(1, 1, 1, 2)
+        scores(1, 1, 1, (0, 1))
+        weigh(0, 1, 1, 0)
         empty_bank(1, low)
         sigmoid(2, PAIR[0])
         sigmoid(2, PAIR[1])
@@ -377,14 +374,14 @@ def tile_rows_a_relu_mask_gate_kernel(tc, qT, kT, t, v, mask, og, out):
         weigh_pool(1, low)
         weigh(1, 1, 0, 0)
         weigh(1, 1, 1, 0)
-        weigh_rest(1, high)
         finish_chunk(0, 0)
+        weigh_rest(1, high)
         finish_chunk(1, 1)
-        finish_part(0, 0, 0, 2, 2)
         quant_w(1, 1, 0, 2)
         values(1, 0, 2, 0)
         quant_pool(0, 2)
         values(1, 2, 4, 1)
+        finish_part(0, 0, 0, 2, 2)
         finish_part(0, 1, 0, 2, 2)
         finish_part(1, 0, 0, 2, 0)
         finish_part(1, 1, 0, 2, 1)

@@ -19,6 +19,7 @@ PACK = 4
 QC = 128
 K_SPLIT = 84
 SCORE_BANKS = (3, 2)
+POOL_SHARE = 80
 HEADS = ((1, 2), (0, 3))
 PAIR = (slice(1, 3), slice(0, 4, 3))
 MASK_PIECES = ((0, 2), (256, 2))
@@ -192,12 +193,12 @@ def tile_rows_a_relu_mask_gate_kernel(tc, qT, kT, t, v, mask, og, out):
 
         def weigh_pool(e, part):
             nc.gpsimd.tensor_tensor(
-                out=w_bf[0, 1][:, e, part], in0=relu_sb[e][:, part], in1=mt[1, e][:, part], op=ALU.mult
+                out=v_bf[:, e, part], in0=relu_sb[e][:, part], in1=mt[1, e][:, part], op=ALU.mult
             )
 
         def weigh_rest(e, part):
             nc.vector.scalar_tensor_tensor(
-                out=w_bf[0, 1][:, e, part],
+                out=v_bf[:, e, part],
                 in0=held[1, 1, e, 1][:, :, part].rearrange("p r q -> p q r"),
                 scalar=0.0,
                 in1=mt[1, e][:, part],
@@ -210,7 +211,7 @@ def tile_rows_a_relu_mask_gate_kernel(tc, qT, kT, t, v, mask, og, out):
             nc.vector.quantize_mx(
                 out=w_codes[1, 1][:, part].bitcast(FP8X4),
                 scales=w_scales[1, 1][:, part],
-                in_=w_bf[0, 1][:, e0:e1].rearrange("p s q r -> p (s q r)"),
+                in_=v_bf[:, e0:e1].rearrange("p s q r -> p (s q r)"),
             )
 
         def quant_w(a, u, s0, s1):
@@ -288,6 +289,7 @@ def tile_rows_a_relu_mask_gate_kernel(tc, qT, kT, t, v, mask, og, out):
 
         every = slice(0, H)
         low, high, whole = slice(0, QC // 2), slice(QC // 2, QC), slice(0, QC)
+        pool_part, rest = slice(0, POOL_SHARE), slice(POOL_SHARE, QC)
         nc.sync.dma_start(out=k_raw[:], in_=kT.rearrange("g (p j) n -> (g p) j n", j=PACK))
         nc.scalar.dma_start(out=t_sb[:], in_=t.rearrange("(s r) o -> s (r o)", r=PACK))
         load_q_inner(0)
@@ -337,11 +339,10 @@ def tile_rows_a_relu_mask_gate_kernel(tc, qT, kT, t, v, mask, og, out):
         scores(1, 0, 0, (0,))
         scores(1, 0, 0, (1,))
         weigh(0, 0, 1, 1)
-        quant_w(0, 0, 0, 2)
         quant_q(1, 0, 1, 2)
         scores(1, 0, 1, (0, 1))
+        quant_w(0, 0, 0, 4)
         weigh(1, 0, 0, 0)
-        quant_w(0, 0, 2, 4)
         weigh(1, 0, 0, 1)
         quant_q(0, 1, 0, 2)
         scores(0, 1, 0, (0, 1))
@@ -355,14 +356,14 @@ def tile_rows_a_relu_mask_gate_kernel(tc, qT, kT, t, v, mask, og, out):
         weigh(0, 1, 0, 1)
         quant_q(1, 1, 0, 1)
         scores(1, 1, 0, (0, 1))
-        sigmoid(0, every)
         empty_bank(0, whole)
+        sigmoid(0, every)
         sigmoid(1, every)
         weigh(0, 1, 1, 1)
         quant_q(1, 1, 1, 2)
         scores(1, 1, 1, (0, 1))
         weigh(0, 1, 1, 0)
-        empty_bank(1, low)
+        empty_bank(1, pool_part)
         sigmoid(2, PAIR[0])
         sigmoid(2, PAIR[1])
         quant_v()
@@ -371,11 +372,11 @@ def tile_rows_a_relu_mask_gate_kernel(tc, qT, kT, t, v, mask, og, out):
         quant_w(0, 1, 0, 4)
         values(0, 0, 4, 2)
         weigh_pool(0, whole)
-        weigh_pool(1, low)
+        weigh_pool(1, pool_part)
         weigh(1, 1, 0, 0)
         weigh(1, 1, 1, 0)
         finish_chunk(0, 0)
-        weigh_rest(1, high)
+        weigh_rest(1, rest)
         finish_chunk(1, 1)
         quant_w(1, 1, 0, 2)
         values(1, 0, 2, 0)

@@ -76,10 +76,10 @@ def tile_rows_a_relu_mask_gate_kernel(tc, qT, kT, t, v, mask, og, out):
             rows = qT[1:3].rearrange("g (p j) q -> (g p) j q", j=PACK)
             nc.sync.dma_start(out=q_half[0, u][:], in_=rows[:, :, half_cols(u)])
 
-        def load_q_outer(dst, part):
+        def load_q_outer(dst, part, places=slice(0, PACK)):
             for g in range(2):
                 rows = qT[HEADS[1][g]].rearrange("(p j) q -> p j q", j=PACK)
-                nc.sync.dma_start(out=dst[ROWS * g : ROWS * (g + 1)], in_=rows[:, :, part])
+                nc.sync.dma_start(out=dst[ROWS * g : ROWS * (g + 1), places], in_=rows[:, places, part])
 
         def load_mask(i):
             q0, n = MASK_PIECES[i]
@@ -300,7 +300,8 @@ def tile_rows_a_relu_mask_gate_kernel(tc, qT, kT, t, v, mask, og, out):
         nc.scalar.activation(out=warm[:, 1:2], in_=warm[:, 0:1], func=ACT.Sigmoid)
         load_q_inner(1)
         load_mask(1)
-        load_q_outer(q_half[1, 1], half_cols(1))
+        load_q_outer(q_half[1, 1], half_cols(1), slice(0, 2))
+        load_q_outer(q_half[1, 1], half_cols(1), slice(2, 4))
         load_v()
         load_og(0, every)
         load_og(1, every)
@@ -366,10 +367,11 @@ def tile_rows_a_relu_mask_gate_kernel(tc, qT, kT, t, v, mask, og, out):
         empty_bank(1, pool_part)
         sigmoid(2, PAIR[0])
         sigmoid(2, PAIR[1])
+        quant_w(0, 1, 2, 4)
         quant_v()
         values_chunk(0, 0)
         values_chunk(1, 1)
-        quant_w(0, 1, 0, 4)
+        quant_w(0, 1, 0, 2)
         values(0, 0, 4, 2)
         weigh_pool(0, whole)
         weigh_pool(1, pool_part)

@@ -305,8 +305,7 @@ def tile_rows_a_relu_mask_gate_kernel(tc, qT, kT, t, v, mask, og, out):
         load_v()
         load_og(0, every)
         load_og(1, every)
-        load_og(2, PAIR[0])
-        load_og(2, PAIR[1])
+        load_og(2, every)
         cast_keys()
         quant_k(0, 2)
         cast_first(0, 0, nc.vector.tensor_copy)
@@ -365,8 +364,7 @@ def tile_rows_a_relu_mask_gate_kernel(tc, qT, kT, t, v, mask, og, out):
         scores(1, 1, 1, (0, 1))
         weigh(0, 1, 1, 0)
         empty_bank(1, pool_part)
-        sigmoid(2, PAIR[0])
-        sigmoid(2, PAIR[1])
+        sigmoid(2, every)
         quant_w(0, 1, 2, 4)
         quant_v()
         values_chunk(0, 0)

@@ -294,14 +294,18 @@ def tile_rows_a_relu_mask_gate_kernel(tc, qT, kT, t, v, mask, og, out):
         nc.scalar.dma_start(out=t_sb[:], in_=t.rearrange("(s r) o -> s (r o)", r=PACK))
         load_q_inner(0)
         load_mask(0)
-        load_q_outer(q_piece[0], cols(0))
-        load_q_outer(q_piece[1], cols(1))
+        load_q_outer(q_piece[0], cols(0), slice(0, 2))
+        load_q_outer(q_piece[0], cols(0), slice(2, 4))
+        load_q_outer(q_piece[1], cols(1), slice(0, 2))
+        load_q_outer(q_piece[1], cols(1), slice(2, 4))
         nc.vector.memset(warm[:, 0:1], 0.0)
         nc.scalar.activation(out=warm[:, 1:2], in_=warm[:, 0:1], func=ACT.Sigmoid)
         load_q_inner(1)
         load_mask(1)
-        load_q_outer(q_half[1, 1], half_cols(1), slice(0, 2))
-        load_q_outer(q_half[1, 1], half_cols(1), slice(2, 4))
+        load_q_outer(q_half[1, 1], half_cols(1), slice(0, 1))
+        load_q_outer(q_half[1, 1], half_cols(1), slice(1, 2))
+        load_q_outer(q_half[1, 1], half_cols(1), slice(2, 3))
+        load_q_outer(q_half[1, 1], half_cols(1), slice(3, 4))
         load_v()
         load_og(0, every)
         load_og(1, every)

@@ -19,7 +19,8 @@ PACK = 4
 QC = 128
 K_SPLIT = 84
 SCORE_BANKS = (3, 2)
-POOL_SHARE = 80
+POOL_SHARE = 64
+MID_SHARE = 64
 HEADS = ((1, 2), (0, 3))
 PAIR = (slice(1, 3), slice(0, 4, 3))
 MASK_PIECES = ((0, 2), (256, 2))
@@ -58,8 +59,10 @@ def tile_rows_a_relu_mask_gate_kernel(tc, qT, kT, t, v, mask, og, out):
         gate = [tile("gate%d" % i, [P, H, n * E], F32) for i, n in enumerate((1, 1, 2))]
         res = [tile("res%d" % i, [P, H, n * E], F32) for i, n in enumerate((1, 1, 2))]
         m_raw = [tile("m_raw%d" % i, [P, PACK, n * QC], F32) for i, (q0, n) in enumerate(MASK_PIECES)]
-        m_scaled = [tile("m_scaled%d" % u, [P, PACK, (u + 1) * QC], F32) for u in range(2)]
-        mt = {x: tile("mt%d%d" % x, [P, QC, PACK], F32) for x in halves}
+        m_scaled = [tile("m_scaled%d" % u, [P, PACK, QC], F32) for u in range(2)]
+        mt = {x: tile("mt%d%d" % x, [P, QC, PACK], F32)[:] for x in halves if x != (1, 1)}
+        mt[1, 1] = q_bf[0, 1][:].rearrange("p e q j -> p (e q j)").bitcast(F32).rearrange("p (q r) -> p q r", r=PACK)
+        relu_mid = tile("relu_mid", [P, MID_SHARE, PACK], F32)
         relu_sb = [tile("relu_sb%d" % e, [P, QC, PACK], F32) for e in range(2)]
         score_banks = [
             [ps.tile([P, PACK, QC], F32, name="score%d%d" % (g, b)) for b in range(SCORE_BANKS[g])] for g in range(2)
@@ -191,6 +194,22 @@ def tile_rows_a_relu_mask_gate_kernel(tc, qT, kT, t, v, mask, og, out):
                 out=relu_sb[e][:, part], in_=held[1, 1, e, 1][:, :, part].rearrange("p r q -> p q r"), func=ACT.Relu
             )
 
+        def mt_pool():
+            nc.gpsimd.tensor_tensor(
+                out=mt[1, 1].rearrange("p (c i) r -> p c r i", i=2),
+                in0=m_raw[1][:, :, 1::2].rearrange("p r (c i) -> p c r i", i=2),
+                in1=t_sb[:, 0:PACK].unsqueeze(1).unsqueeze(3).to_broadcast([P, QC // 2, PACK, 2]),
+                op=ALU.mult,
+            )
+
+        def empty_mid():
+            src = held[0, 1, 0, 1][:, :, 0:MID_SHARE].rearrange("p r q -> p q r")
+            nc.scalar.activation(out=relu_mid[:], in_=src, func=ACT.Relu)
+
+        def weigh_mid():
+            dst = w_bf[0, 1][:, slot(1, 0, 1), 0:MID_SHARE]
+            nc.gpsimd.tensor_tensor(out=dst, in0=relu_mid[:], in1=mt[1, 0][:, 0:MID_SHARE], op=ALU.mult)
+
         def weigh_pool(e, part):
             nc.gpsimd.tensor_tensor(
                 out=v_bf[:, e, part], in0=relu_sb[e][:, part], in1=mt[1, e][:, part], op=ALU.mult
@@ -321,12 +340,7 @@ def tile_rows_a_relu_mask_gate_kernel(tc, qT, kT, t, v, mask, og, out):
         cast_first(1, 1, nc.scalar.copy)
         cast_dealt_both(0)
         scale_dealt(0)
-        scale_dealt(1)
         weave_mask(1, 0)
-        weave_mask(1, 1)
-        cast_dealt(1, 0)
-        cast_dealt(1, 1)
-        cast_v()
         quant_q(0, 0, 0, 1)
         scores(0, 0, 0, (0,))
         scores(0, 0, 0, (1,))
@@ -350,22 +364,27 @@ def tile_rows_a_relu_mask_gate_kernel(tc, qT, kT, t, v, mask, og, out):
         weigh(1, 0, 0, 1)
         quant_q(0, 1, 0, 2)
         scores(0, 1, 0, (0, 1))
-        weigh(1, 0, 1, 0)
-        scores(0, 1, 1, (0,))
-        weigh(1, 0, 1, 1)
-        scores(0, 1, 1, (1,))
+        mt_pool()
+        empty_mid()
+        weigh_mid()
+        cast_dealt(1, 0)
+        cast_dealt(1, 1)
+        cast_v()
         quant_w(1, 0, 0, 2)
-        quant_w(1, 0, 2, 4)
+        weigh(1, 0, 1, 1)
+        scores(0, 1, 1, (0, 1))
+        weigh(1, 0, 1, 0)
         weigh(0, 1, 0, 0)
-        weigh(0, 1, 0, 1)
+        weigh(0, 1, 0, 1, slice(MID_SHARE, QC))
+        weigh(0, 1, 1, 1)
         quant_q(1, 1, 0, 1)
         scores(1, 1, 0, (0, 1))
+        quant_w(1, 0, 2, 4)
+        quant_q(1, 1, 1, 2)
+        scores(1, 1, 1, (0, 1))
         empty_bank(0, whole)
         sigmoid(0, every)
         sigmoid(1, every)
-        weigh(0, 1, 1, 1)
-        quant_q(1, 1, 1, 2)
-        scores(1, 1, 1, (0, 1))
         weigh(0, 1, 1, 0)
         empty_bank(1, pool_part)
         sigmoid(2, every)

@@ -330,9 +330,10 @@ def tile_rows_a_relu_mask_gate_kernel(tc, qT, kT, t, v, mask, og, out):
         load_og(1, every)
         load_og(2, every)
         cast_keys()
-        quant_k(0, 2)
         cast_first(0, 0, nc.vector.tensor_copy)
         cast_first(0, 1, nc.scalar.copy)
+        quant_k(0, 2)
+        quant_q(0, 0, 0, 1)
         quant_k(2, 4)
         scale_first()
         weave_mask(0, 1)
@@ -341,7 +342,6 @@ def tile_rows_a_relu_mask_gate_kernel(tc, qT, kT, t, v, mask, og, out):
         cast_dealt_both(0)
         scale_dealt(0)
         weave_mask(1, 0)
-        quant_q(0, 0, 0, 1)
         scores(0, 0, 0, (0,))
         scores(0, 0, 0, (1,))
         quant_q(0, 0, 1, 2)

@@ -34,7 +34,7 @@ def tile_rows_a_relu_mask_gate_kernel(tc, qT, kT, t, v, mask, og, out):
         ctx.enter_context(tc.manual_schedule())
 
         def tile(name, shape, dtype):
-            return sb.tile(shape, dtype, name=name, align_bytes=64)
+            return sb.tile(shape, dtype, name=name, align_bytes=256)
 
         t_sb = tile("t_sb", [P, PACK], F32)
         warm = tile("warm", [P, 2], F32)

@@ -342,11 +342,9 @@ def tile_rows_a_relu_mask_gate_kernel(tc, qT, kT, t, v, mask, og, out):
         cast_dealt_both(0)
         scale_dealt(0)
         weave_mask(1, 0)
-        scores(0, 0, 0, (0,))
-        scores(0, 0, 0, (1,))
+        scores(0, 0, 0, (0, 1))
         quant_q(0, 0, 1, 2)
-        scores(0, 0, 1, (0,))
-        scores(0, 0, 1, (1,))
+        scores(0, 0, 1, (0, 1))
         mt_vector(0, low)
         mt_vector(0, high)
         weigh(0, 0, 0, 0, low)
@@ -354,8 +352,7 @@ def tile_rows_a_relu_mask_gate_kernel(tc, qT, kT, t, v, mask, og, out):
         weigh(0, 0, 0, 1)
         weigh(0, 0, 1, 0)
         quant_q(1, 0, 0, 1)
-        scores(1, 0, 0, (0,))
-        scores(1, 0, 0, (1,))
+        scores(1, 0, 0, (0, 1))
         weigh(0, 0, 1, 1)
         quant_q(1, 0, 1, 2)
         scores(1, 0, 1, (0, 1))

@@ -64,6 +64,9 @@ def tile_rows_a_relu_mask_gate_kernel(tc, qT, kT, t, v, mask, og, out):
         mt[1, 1] = q_bf[0, 1][:].rearrange("p e q j -> p (e q j)").bitcast(F32).rearrange("p (q r) -> p q r", r=PACK)
         relu_mid = tile("relu_mid", [P, MID_SHARE, PACK], F32)
         relu_sb = [tile("relu_sb%d" % e, [P, QC, PACK], F32) for e in range(2)]
+        pool_in = tile("pool_in", [P, 16], F32)
+        pool_f32 = tile("pool_f32", [P, 16], F32)
+        pool_bf = tile("pool_bf", [P, 16], BF16)
         score_banks = [
             [ps.tile([P, PACK, QC], F32, name="score%d%d" % (g, b)) for b in range(SCORE_BANKS[g])] for g in range(2)
         ]
@@ -319,6 +322,9 @@ def tile_rows_a_relu_mask_gate_kernel(tc, qT, kT, t, v, mask, og, out):
         load_q_outer(q_piece[1], cols(1), slice(2, 4))
         nc.vector.memset(warm[:, 0:1], 0.0)
         nc.scalar.activation(out=warm[:, 1:2], in_=warm[:, 0:1], func=ACT.Sigmoid)
+        nc.gpsimd.memset(pool_in[:], 1.0)
+        nc.gpsimd.tensor_tensor(out=pool_f32[:], in0=pool_in[:], in1=pool_in[:], op=ALU.mult)
+        nc.gpsimd.tensor_tensor(out=pool_bf[:], in0=pool_in[:], in1=pool_in[:], op=ALU.mult)
         load_q_inner(1)
         load_mask(1)
         load_q_outer(q_half[1, 1], half_cols(1), slice(0, 1))

@@ -19,11 +19,10 @@ PACK = 4
 QC = 128
 K_SPLIT = 84
 SCORE_BANKS = (3, 2)
-POOL_SHARE = 64
-MID_SHARE = 64
+MID_SHARE = 32
+LAST_SHARE = 64
 HEADS = ((1, 2), (0, 3))
 PAIR = (slice(1, 3), slice(0, 4, 3))
-MASK_PIECES = ((0, 2), (256, 2))
 
 
 def tile_rows_a_relu_mask_gate_kernel(tc, qT, kT, t, v, mask, og, out):
@@ -49,7 +48,9 @@ def tile_rows_a_relu_mask_gate_kernel(tc, qT, kT, t, v, mask, og, out):
         halves = [(a, u) for a in range(2) for u in range(2)]
         q_half = {x: tile("q_half%d%d" % x, [P, PACK, 2 * QC], F32) for x in halves if x != (1, 0)}
         q_piece = [tile("q_piece%d" % e, [P, PACK, QC], F32) for e in range(2)]
-        q_bf = {x: tile("q_bf%d%d" % x, [P, 2, QC, PACK], BF16) for x in halves}
+        q_bf = {x: tile("q_bf%d%d" % x, [P, 2, QC, PACK], BF16) for x in halves if x != (1, 0)}
+        shared = tile("shared", [P, 3, QC, PACK], BF16)
+        q_bf[1, 0] = shared[:, 0::2]
         q_codes = {x: tile("q_codes%d%d" % x, [P, 2 * QC], I32) for x in halves}
         q_scales = {x: tile("q_scales%d%d" % x, [P, 2 * QC], U8) for x in halves}
         w_bf = {x: tile("w_bf%d%d" % x, [P, 4, QC, PACK], BF16) for x in halves}
@@ -58,12 +59,10 @@ def tile_rows_a_relu_mask_gate_kernel(tc, qT, kT, t, v, mask, og, out):
         og_raw = [tile("og_raw%d" % i, [P, H, n * E], F32) for i, n in enumerate((1, 1, 2))]
         gate = [tile("gate%d" % i, [P, H, n * E], F32) for i, n in enumerate((1, 1, 2))]
         res = [tile("res%d" % i, [P, H, n * E], F32) for i, n in enumerate((1, 1, 2))]
-        m_raw = [tile("m_raw%d" % i, [P, PACK, n * QC], F32) for i, (q0, n) in enumerate(MASK_PIECES)]
+        m_raw = [tile("m_raw%d" % u, [P, PACK, 2 * QC], F32) for u in range(2)]
         m_scaled = [tile("m_scaled%d" % u, [P, PACK, QC], F32) for u in range(2)]
         mt = {x: tile("mt%d%d" % x, [P, QC, PACK], F32)[:] for x in halves if x != (1, 1)}
-        mt[1, 1] = q_bf[0, 1][:].rearrange("p e q j -> p (e q j)").bitcast(F32).rearrange("p (q r) -> p q r", r=PACK)
-        relu_mid = tile("relu_mid", [P, MID_SHARE, PACK], F32)
-        relu_sb = [tile("relu_sb%d" % e, [P, QC, PACK], F32) for e in range(2)]
+        relu_sb = [tile("relu_sb%d" % i, [P, QC, PACK], F32) for i in range(4)]
         pool_in = tile("pool_in", [P, 16], F32)
         pool_f32 = tile("pool_f32", [P, 16], F32)
         pool_bf = tile("pool_bf", [P, 16], BF16)
@@ -78,23 +77,32 @@ def tile_rows_a_relu_mask_gate_kernel(tc, qT, kT, t, v, mask, og, out):
         def half_cols(u):
             return slice(2 * u * QC, 2 * (u + 1) * QC)
 
+        def slot(u, e, g):
+            return 2 * e + g if u == 0 else 2 * g + e
+
+        stage = {(a, u, e, g): w_bf[a, u][:, slot(u, e, g)] for a, u in halves for e in range(2) for g in range(2)}
+
+        def as_mask(buf):
+            return buf.rearrange("p e q j -> p (e q j)").bitcast(F32).rearrange("p (q r) -> p q r", r=PACK)
+
+        stage[0, 0, 1, 0] = shared[:, 1]
+        stage[0, 0, 1, 1] = shared[:, 2]
+        mt[1, 1] = as_mask(shared[:, 1:3])
+        stage[1, 1, 0, 1] = v_bf[:, 0]
+        stage[1, 1, 1, 1] = v_bf[:, 1]
+
         def load_q_inner(u):
             rows = qT[1:3].rearrange("g (p j) q -> (g p) j q", j=PACK)
             nc.sync.dma_start(out=q_half[0, u][:], in_=rows[:, :, half_cols(u)])
 
-        def load_q_outer(dst, part, places=slice(0, PACK)):
+        def load_q_outer(dst, part, places):
             for g in range(2):
                 rows = qT[HEADS[1][g]].rearrange("(p j) q -> p j q", j=PACK)
                 nc.sync.dma_start(out=dst[ROWS * g : ROWS * (g + 1), places], in_=rows[:, places, part])
 
-        def load_mask(i):
-            q0, n = MASK_PIECES[i]
+        def load_mask(u):
             rows = mask.rearrange("(s r) q -> s r q", r=PACK)
-            nc.sync.dma_start(out=m_raw[i][:], in_=rows[:, :, q0 : q0 + n * QC])
-
-        def first_mask(e):
-            i = max(x for x, (q0, n) in enumerate(MASK_PIECES) if q0 <= e * QC)
-            return m_raw[i][:, :, e * QC - MASK_PIECES[i][0] : (e + 1) * QC - MASK_PIECES[i][0]]
+            nc.sync.dma_start(out=m_raw[u][:], in_=rows[:, :, half_cols(u)])
 
         def rows_of(x, i):
             part = cols(i) if i < 2 else half_cols(1)
@@ -106,6 +114,19 @@ def tile_rows_a_relu_mask_gate_kernel(tc, qT, kT, t, v, mask, og, out):
         def load_v():
             nc.sync.dma_start(
                 out=v_raw[:].rearrange("p g j e -> p g (j e)"), in_=v.rearrange("g (p j) e -> p g (j e)", j=PACK)
+            )
+
+        def cast_keys():
+            k_src = k_raw[:].rearrange("p j (s r) -> p s j r", r=PACK)
+            k_dst = k_bf[:].rearrange("p r s j -> p s j r")
+            nc.vector.tensor_copy(out=k_dst[:, :K_SPLIT], in_=k_src[:, :K_SPLIT])
+            nc.scalar.copy(out=k_dst[:, K_SPLIT:], in_=k_src[:, K_SPLIT:])
+
+        def quant_k(i):
+            nc.vector.quantize_mx(
+                out=k_codes[:, half_cols(i)].bitcast(FP8X4),
+                scales=k_scales[:, half_cols(i)],
+                in_=k_bf[:, 2 * i : 2 * i + 2].rearrange("p r s j -> p (r s j)"),
             )
 
         def cast_first(a, e, copy):
@@ -135,28 +156,27 @@ def tile_rows_a_relu_mask_gate_kernel(tc, qT, kT, t, v, mask, og, out):
                 in_=q_bf[a, u][:, e0:e1].rearrange("p e q j -> p (e q j)"),
             )
 
-        def mt_vector(e, part):
-            nc.vector.tensor_tensor(
-                out=mt[0, e][:, part].rearrange("p (c i) r -> p c r i", i=2),
-                in0=first_mask(e)[:, :, part].rearrange("p r (c i) -> p c r i", i=2),
+        def mask_rows(u, e):
+            return m_raw[0][:, :, cols(e)] if u == 0 else m_raw[1][:, :, e::2]
+
+        def mask_times_t(engine, u, e, part):
+            engine.tensor_tensor(
+                out=mt[u, e][:, part].rearrange("p (c i) r -> p c r i", i=2),
+                in0=mask_rows(u, e)[:, :, part].rearrange("p r (c i) -> p c r i", i=2),
                 in1=t_sb[:, 0:PACK].unsqueeze(1).unsqueeze(3).to_broadcast([P, (part.stop - part.start) // 2, PACK, 2]),
                 op=ALU.mult,
             )
 
-        def scale_mask(src, dst):
+        def scale_mask(u, e):
             for r in range(PACK):
-                nc.scalar.activation(out=dst[:, r], in_=src[:, r], func=ACT.Copy, scale=t_sb[:, r : r + 1])
+                nc.scalar.activation(
+                    out=m_scaled[u][:, r], in_=mask_rows(u, e)[:, r], func=ACT.Copy, scale=t_sb[:, r : r + 1]
+                )
 
-        def scale_first():
-            scale_mask(first_mask(1), m_scaled[0][:])
-
-        def scale_dealt(e):
-            scale_mask(m_raw[-1][:, :, e::2], m_scaled[1][:, :, cols(e)])
-
-        def weave_mask(u, e):
-            src = m_scaled[0][:] if u == 0 else m_scaled[1][:, :, cols(e)]
+        def weave_mask(u, e, part=slice(0, QC)):
             nc.scalar.copy(
-                out=mt[u, e][:].rearrange("p (c i) r -> p c r i", i=2), in_=src.rearrange("p r (c i) -> p c r i", i=2)
+                out=mt[u, e][:, part].rearrange("p (c i) r -> p c r i", i=2),
+                in_=m_scaled[u][:, :, part].rearrange("p r (c i) -> p c r i", i=2),
             )
 
         turn = [0, 0]
@@ -171,20 +191,17 @@ def tile_rows_a_relu_mask_gate_kernel(tc, qT, kT, t, v, mask, og, out):
                     rows = slice(ROWS * g, ROWS * (g + 1))
                     nc.tensor.matmul_mx(
                         out=held[a, u, e, g][:, r, :],
-                        lhsT=k_codes[rows, r * P : (r + 1) * P].bitcast(FP8X4),
-                        lhsT_scale=k_scales[rows, r * P : (r + 1) * P],
+                        lhsT=k_codes[rows, cols(r)].bitcast(FP8X4),
+                        lhsT_scale=k_scales[rows, cols(r)],
                         rhs=q_codes[a, u][rows, cols(e)].bitcast(FP8X4),
                         rhs_scale=q_scales[a, u][rows, cols(e)],
                         start=True,
                         stop=True,
                     )
 
-        def slot(u, e, g):
-            return 2 * e + g if u == 0 else 2 * g + e
-
         def weigh(a, u, e, g, part=slice(0, QC)):
             nc.vector.scalar_tensor_tensor(
-                out=w_bf[a, u][:, slot(u, e, g), part],
+                out=stage[a, u, e, g][:, part],
                 in0=held[a, u, e, g][:, :, part].rearrange("p r q -> p q r"),
                 scalar=0.0,
                 in1=mt[u, e][:, part],
@@ -192,56 +209,22 @@ def tile_rows_a_relu_mask_gate_kernel(tc, qT, kT, t, v, mask, og, out):
                 op1=ALU.mult,
             )
 
-        def empty_bank(e, part):
-            nc.scalar.activation(
-                out=relu_sb[e][:, part], in_=held[1, 1, e, 1][:, :, part].rearrange("p r q -> p q r"), func=ACT.Relu
-            )
+        def empty_bank(i, a, u, e, g, part=slice(0, QC)):
+            src = held[a, u, e, g][:, :, part].rearrange("p r q -> p q r")
+            nc.scalar.activation(out=relu_sb[i][:, part], in_=src, func=ACT.Relu)
 
-        def mt_pool():
+        def weigh_pool(i, a, u, e, g, part=slice(0, QC)):
             nc.gpsimd.tensor_tensor(
-                out=mt[1, 1].rearrange("p (c i) r -> p c r i", i=2),
-                in0=m_raw[1][:, :, 1::2].rearrange("p r (c i) -> p c r i", i=2),
-                in1=t_sb[:, 0:PACK].unsqueeze(1).unsqueeze(3).to_broadcast([P, QC // 2, PACK, 2]),
-                op=ALU.mult,
+                out=stage[a, u, e, g][:, part], in0=relu_sb[i][:, part], in1=mt[u, e][:, part], op=ALU.mult
             )
 
-        def empty_mid():
-            src = held[0, 1, 0, 1][:, :, 0:MID_SHARE].rearrange("p r q -> p q r")
-            nc.scalar.activation(out=relu_mid[:], in_=src, func=ACT.Relu)
-
-        def weigh_mid():
-            dst = w_bf[0, 1][:, slot(1, 0, 1), 0:MID_SHARE]
-            nc.gpsimd.tensor_tensor(out=dst, in0=relu_mid[:], in1=mt[1, 0][:, 0:MID_SHARE], op=ALU.mult)
-
-        def weigh_pool(e, part):
-            nc.gpsimd.tensor_tensor(
-                out=v_bf[:, e, part], in0=relu_sb[e][:, part], in1=mt[1, e][:, part], op=ALU.mult
-            )
-
-        def weigh_rest(e, part):
-            nc.vector.scalar_tensor_tensor(
-                out=v_bf[:, e, part],
-                in0=held[1, 1, e, 1][:, :, part].rearrange("p r q -> p q r"),
-                scalar=0.0,
-                in1=mt[1, e][:, part],
-                op0=ALU.max,
-                op1=ALU.mult,
-            )
-
-        def quant_pool(e0, e1):
-            part = slice((2 + e0) * QC, (2 + e1) * QC)
-            nc.vector.quantize_mx(
-                out=w_codes[1, 1][:, part].bitcast(FP8X4),
-                scales=w_scales[1, 1][:, part],
-                in_=v_bf[:, e0:e1].rearrange("p s q r -> p (s q r)"),
-            )
-
-        def quant_w(a, u, s0, s1):
+        def quant_w(a, u, s0, s1, src=None):
             part = slice(s0 * QC, s1 * QC)
+            src = w_bf[a, u][:, s0:s1] if src is None else src
             nc.vector.quantize_mx(
                 out=w_codes[a, u][:, part].bitcast(FP8X4),
                 scales=w_scales[a, u][:, part],
-                in_=w_bf[a, u][:, s0:s1].rearrange("p s q r -> p (s q r)"),
+                in_=src.rearrange("p s q r -> p (s q r)"),
             )
 
         def value_pass(a, u, e, g, y):
@@ -279,11 +262,10 @@ def tile_rows_a_relu_mask_gate_kernel(tc, qT, kT, t, v, mask, og, out):
             gated(res[2][:, PAIR[a]], y_banks[b][:].rearrange("p (g f) -> p g f", g=2), gate[2][:, PAIR[a]])
             nc.sync.dma_start(out=rows_of(out, 2)[:, PAIR[a]], in_=res[2][:, PAIR[a]])
 
-        def finish_part(a, g, e0, e1, b):
+        def finish_head(a, g, b):
             h = HEADS[a][g]
-            part = slice(e0 * E, e1 * E)
-            gated(res[2][:, h, part], y_banks[b][:, (2 * g + e0) * E : (2 * g + e1) * E], gate[2][:, h, part])
-            nc.sync.dma_start(out=rows_of(out, 2)[:, h, part], in_=res[2][:, h, part])
+            gated(res[2][:, h], y_banks[b][:, 2 * g * E : 2 * (g + 1) * E], gate[2][:, h])
+            nc.sync.dma_start(out=rows_of(out, 2)[:, h], in_=res[2][:, h])
 
         def cast_v():
             nc.scalar.copy(
@@ -296,22 +278,10 @@ def tile_rows_a_relu_mask_gate_kernel(tc, qT, kT, t, v, mask, og, out):
                 out=v_codes[:].bitcast(FP8X4), scales=v_scales[:], in_=v_bf[:].rearrange("p g e j -> p (g e j)")
             )
 
-        def cast_keys():
-            k_src = k_raw[:].rearrange("p j (s r) -> p s j r", r=PACK)
-            k_dst = k_bf[:].rearrange("p r s j -> p s j r")
-            nc.vector.tensor_copy(out=k_dst[:, :K_SPLIT], in_=k_src[:, :K_SPLIT])
-            nc.scalar.copy(out=k_dst[:, K_SPLIT:], in_=k_src[:, K_SPLIT:])
-
-        def quant_k(r0, r1):
-            nc.vector.quantize_mx(
-                out=k_codes[:, r0 * P : r1 * P].bitcast(FP8X4),
-                scales=k_scales[:, r0 * P : r1 * P],
-                in_=k_bf[:, r0:r1].rearrange("p r s j -> p (r s j)"),
-            )
-
         every = slice(0, H)
         low, high, whole = slice(0, QC // 2), slice(QC // 2, QC), slice(0, QC)
-        pool_part, rest = slice(0, POOL_SHARE), slice(POOL_SHARE, QC)
+        mid, mid_rest = slice(0, MID_SHARE), slice(MID_SHARE, QC)
+        last, last_rest = slice(0, LAST_SHARE), slice(LAST_SHARE, QC)
         nc.sync.dma_start(out=k_raw[:], in_=kT.rearrange("g (p j) n -> (g p) j n", j=PACK))
         nc.scalar.dma_start(out=t_sb[:], in_=t.rearrange("(s r) o -> s (r o)", r=PACK))
         load_q_inner(0)
@@ -338,58 +308,62 @@ def tile_rows_a_relu_mask_gate_kernel(tc, qT, kT, t, v, mask, og, out):
         cast_keys()
         cast_first(0, 0, nc.vector.tensor_copy)
         cast_first(0, 1, nc.scalar.copy)
-        quant_k(0, 2)
+        quant_k(0)
         quant_q(0, 0, 0, 1)
-        quant_k(2, 4)
-        scale_first()
-        weave_mask(0, 1)
-        cast_first(1, 0, nc.scalar.copy)
-        cast_first(1, 1, nc.scalar.copy)
-        cast_dealt_both(0)
-        scale_dealt(0)
-        weave_mask(1, 0)
+        quant_k(1)
         scores(0, 0, 0, (0, 1))
         quant_q(0, 0, 1, 2)
         scores(0, 0, 1, (0, 1))
-        mt_vector(0, low)
-        mt_vector(0, high)
+
+        scale_mask(0, 1)
+        cast_first(1, 0, nc.scalar.copy)
+        weave_mask(0, 1)
+        cast_first(1, 1, nc.scalar.copy)
+        mask_times_t(nc.vector, 0, 0, low)
+        mask_times_t(nc.vector, 0, 0, high)
         weigh(0, 0, 0, 0, low)
         weigh(0, 0, 0, 0, high)
         weigh(0, 0, 0, 1)
-        weigh(0, 0, 1, 0)
+        empty_bank(0, 0, 0, 1, 1)
+        cast_dealt_both(0)
+        scale_mask(1, 0)
+        weave_mask(1, 0)
         quant_q(1, 0, 0, 1)
         scores(1, 0, 0, (0, 1))
-        weigh(0, 0, 1, 1)
+        quant_w(0, 0, 0, 2)
+        weigh(0, 0, 1, 0)
         quant_q(1, 0, 1, 2)
         scores(1, 0, 1, (0, 1))
-        quant_w(0, 0, 0, 4)
+        weigh_pool(0, 0, 0, 1, 1)
         weigh(1, 0, 0, 0)
         weigh(1, 0, 0, 1)
+        weigh(1, 0, 1, 1)
         quant_q(0, 1, 0, 2)
         scores(0, 1, 0, (0, 1))
-        mt_pool()
-        empty_mid()
-        weigh_mid()
+        quant_w(0, 0, 2, 4, shared[:, 1:3])
+        mask_times_t(nc.gpsimd, 1, 1, whole)
+        quant_w(1, 0, 0, 2)
+        weigh(1, 0, 1, 0)
+        scores(0, 1, 1, (0, 1))
+        empty_bank(3, 0, 1, 0, 1, mid)
+        weigh_pool(3, 0, 1, 0, 1, mid)
         cast_dealt(1, 0)
         cast_dealt(1, 1)
         cast_v()
-        quant_w(1, 0, 0, 2)
-        weigh(1, 0, 1, 1)
-        scores(0, 1, 1, (0, 1))
-        weigh(1, 0, 1, 0)
         weigh(0, 1, 0, 0)
-        weigh(0, 1, 0, 1, slice(MID_SHARE, QC))
+        weigh(0, 1, 0, 1, mid_rest)
         weigh(0, 1, 1, 1)
         quant_q(1, 1, 0, 1)
         scores(1, 1, 0, (0, 1))
         quant_w(1, 0, 2, 4)
         quant_q(1, 1, 1, 2)
         scores(1, 1, 1, (0, 1))
-        empty_bank(0, whole)
+
+        empty_bank(1, 1, 1, 0, 1)
         sigmoid(0, every)
         sigmoid(1, every)
         weigh(0, 1, 1, 0)
-        empty_bank(1, pool_part)
+        empty_bank(2, 1, 1, 1, 1, last)
         sigmoid(2, every)
         quant_w(0, 1, 2, 4)
         quant_v()
@@ -397,18 +371,18 @@ def tile_rows_a_relu_mask_gate_kernel(tc, qT, kT, t, v, mask, og, out):
         values_chunk(1, 1)
         quant_w(0, 1, 0, 2)
         values(0, 0, 4, 2)
-        weigh_pool(0, whole)
-        weigh_pool(1, pool_part)
+        weigh_pool(1, 1, 1, 0, 1)
+        weigh_pool(2, 1, 1, 1, 1, last)
         weigh(1, 1, 0, 0)
         weigh(1, 1, 1, 0)
         finish_chunk(0, 0)
-        weigh_rest(1, rest)
+        weigh(1, 1, 1, 1, last_rest)
         finish_chunk(1, 1)
         quant_w(1, 1, 0, 2)
         values(1, 0, 2, 0)
-        quant_pool(0, 2)
+        quant_w(1, 1, 2, 4, v_bf[:])
         values(1, 2, 4, 1)
-        finish_part(0, 0, 0, 2, 2)
-        finish_part(0, 1, 0, 2, 2)
-        finish_part(1, 0, 0, 2, 0)
-        finish_part(1, 1, 0, 2, 1)
+        finish_head(0, 0, 2)
+        finish_head(0, 1, 2)
+        finish_head(1, 0, 0)
+        finish_head(1, 1, 1)

@@ -248,6 +248,18 @@ def tile_rows_a_relu_mask_gate_kernel(tc, qT, kT, t, v, mask, og, out):
             for s in range(s0, s1):
                 value_pass(a, 1, s % 2, s // 2, y_banks[b][:, cols(s)])
 
+        def warm_tensor():
+            for r in range(PACK):
+                nc.tensor.matmul_mx(
+                    out=y_banks[2][:, cols(r)],
+                    lhsT=k_codes[:, cols(r)].bitcast(FP8X4),
+                    lhsT_scale=k_scales[:, cols(r)],
+                    rhs=q_codes[0, 0][:, cols(0)].bitcast(FP8X4),
+                    rhs_scale=q_scales[0, 0][:, cols(0)],
+                    start=True,
+                    stop=True,
+                )
+
         def sigmoid(i, heads):
             nc.scalar.activation(out=gate[i][:, heads], in_=og_raw[i][:, heads], func=ACT.Sigmoid)
 
@@ -315,6 +327,7 @@ def tile_rows_a_relu_mask_gate_kernel(tc, qT, kT, t, v, mask, og, out):
         quant_q(0, 0, 1, 2)
         scores(0, 0, 1, (0, 1))
 
+        warm_tensor()
         scale_mask(0, 1)
         cast_first(1, 0, nc.scalar.copy)
         weave_mask(0, 1)

from contextlib import ExitStack

import concourse.mybir as mybir

H, KV, D, NQ, N, E = 4, 2, 256, 512, 512, 128
FLOPS = 2 * H * N * NQ * D + 2 * H * NQ * N * E

F32 = mybir.dt.float32
BF16 = mybir.dt.bfloat16
I32 = mybir.dt.int32
U8 = mybir.dt.uint8
FP8X4 = mybir.dt.float8_e4m3fn_x4
ALU = mybir.AluOpType
ACT = mybir.ActivationFunctionType

P = 128
ROWS = 64
PACK = 4
QC = 128
K_SPLIT = 84
SCORE_BANKS = (3, 2)
MID_SHARE = 32
LAST_SHARE = 64
HEADS = ((1, 2), (0, 3))
PAIR = (slice(1, 3), slice(0, 4, 3))


def tile_rows_a_relu_mask_gate_kernel(tc, qT, kT, t, v, mask, og, out):
    nc = tc.nc
    with ExitStack() as ctx:
        sb = ctx.enter_context(tc.tile_pool(name="sb", bufs=1))
        ps = ctx.enter_context(tc.psum_pool(name="ps", bufs=1))
        ctx.enter_context(tc.manual_schedule())

        def tile(name, shape, dtype):
            return sb.tile(shape, dtype, name=name, align_bytes=256)

        t_sb = tile("t_sb", [P, PACK], F32)
        warm = tile("warm", [P, 2], F32)
        k_raw = tile("k_raw", [P, PACK, N], F32)
        k_bf = tile("k_bf", [P, PACK, P, PACK], BF16)
        k_codes = tile("k_codes", [P, N], I32)
        k_scales = tile("k_scales", [P, N], U8)
        v_raw = tile("v_raw", [P, KV, PACK, E], F32)
        v_bf = tile("v_bf", [P, KV, E, PACK], BF16)
        v_codes = tile("v_codes", [P, KV * E], I32)
        v_scales = tile("v_scales", [P, KV * E], U8)
        halves = [(a, u) for a in range(2) for u in range(2)]
        q_half = {x: tile("q_half%d%d" % x, [P, PACK, 2 * QC], F32) for x in halves if x != (1, 0)}
        q_piece = [tile("q_piece%d" % e, [P, PACK, QC], F32) for e in range(2)]
        q_bf = {x: tile("q_bf%d%d" % x, [P, 2, QC, PACK], BF16) for x in halves if x != (1, 0)}
        shared = tile("shared", [P, 3, QC, PACK], BF16)
        q_bf[1, 0] = shared[:, 0::2]
        q_codes = {x: tile("q_codes%d%d" % x, [P, 2 * QC], I32) for x in halves}
        q_scales = {x: tile("q_scales%d%d" % x, [P, 2 * QC], U8) for x in halves}
        w_bf = {x: tile("w_bf%d%d" % x, [P, 4, QC, PACK], BF16) for x in halves}
        w_codes = {x: tile("w_codes%d%d" % x, [P, 4 * QC], I32) for x in halves}
        w_scales = {x: tile("w_scales%d%d" % x, [P, 4 * QC], U8) for x in halves}
        og_raw = [tile("og_raw%d" % i, [P, H, n * E], F32) for i, n in enumerate((1, 1, 2))]
        gate = [tile("gate%d" % i, [P, H, n * E], F32) for i, n in enumerate((1, 1, 2))]
        res = [tile("res%d" % i, [P, H, n * E], F32) for i, n in enumerate((1, 1, 2))]
        m_raw = [tile("m_raw%d" % u, [P, PACK, 2 * QC], F32) for u in range(2)]
        m_scaled = [tile("m_scaled%d" % u, [P, PACK, QC], F32) for u in range(2)]
        mt = {x: tile("mt%d%d" % x, [P, QC, PACK], F32)[:] for x in halves if x != (1, 1)}
        relu_sb = [tile("relu_sb%d" % i, [P, QC, PACK], F32) for i in range(4)]
        pool_in = tile("pool_in", [P, 16], F32)
        pool_f32 = tile("pool_f32", [P, 16], F32)
        pool_bf = tile("pool_bf", [P, 16], BF16)
        score_banks = [
            [ps.tile([P, PACK, QC], F32, name="score%d%d" % (g, b)) for b in range(SCORE_BANKS[g])] for g in range(2)
        ]
        y_banks = [ps.tile([P, PACK * E], F32, name="y%d" % b) for b in range(8 - sum(SCORE_BANKS))]

        def cols(c):
            return slice(c * QC, (c + 1) * QC)

        def half_cols(u):
            return slice(2 * u * QC, 2 * (u + 1) * QC)

        def slot(u, e, g):
            return 2 * e + g if u == 0 else 2 * g + e

        stage = {(a, u, e, g): w_bf[a, u][:, slot(u, e, g)] for a, u in halves for e in range(2) for g in range(2)}

        def as_mask(buf):
            return buf.rearrange("p e q j -> p (e q j)").bitcast(F32).rearrange("p (q r) -> p q r", r=PACK)

        stage[0, 0, 1, 0] = shared[:, 1]
        stage[0, 0, 1, 1] = shared[:, 2]
        mt[1, 1] = as_mask(shared[:, 1:3])
        stage[1, 1, 0, 1] = v_bf[:, 0]
        stage[1, 1, 1, 1] = v_bf[:, 1]

        def load_q_inner(u):
            rows = qT[1:3].rearrange("g (p j) q -> (g p) j q", j=PACK)
            nc.sync.dma_start(out=q_half[0, u][:], in_=rows[:, :, half_cols(u)])

        def load_q_outer(dst, part, places):
            for g in range(2):
                rows = qT[HEADS[1][g]].rearrange("(p j) q -> p j q", j=PACK)
                nc.sync.dma_start(out=dst[ROWS * g : ROWS * (g + 1), places], in_=rows[:, places, part])

        def load_mask(u):
            rows = mask.rearrange("(s r) q -> s r q", r=PACK)
            nc.sync.dma_start(out=m_raw[u][:], in_=rows[:, :, half_cols(u)])

        def rows_of(x, i):
            part = cols(i) if i < 2 else half_cols(1)
            return x[:, part].rearrange("h (m e) f -> m h (e f)", m=QC)

        def load_og(i, heads):
            nc.sync.dma_start(out=og_raw[i][:, heads], in_=rows_of(og, i)[:, heads])

        def load_v():
            nc.sync.dma_start(
                out=v_raw[:].rearrange("p g j e -> p g (j e)"), in_=v.rearrange("g (p j) e -> p g (j e)", j=PACK)
            )

        def cast_keys():
            k_src = k_raw[:].rearrange("p j (s r) -> p s j r", r=PACK)
            k_dst = k_bf[:].rearrange("p r s j -> p s j r")
            nc.vector.tensor_copy(out=k_dst[:, :K_SPLIT], in_=k_src[:, :K_SPLIT])
            nc.scalar.copy(out=k_dst[:, K_SPLIT:], in_=k_src[:, K_SPLIT:])

        def quant_k(i):
            nc.vector.quantize_mx(
                out=k_codes[:, half_cols(i)].bitcast(FP8X4),
                scales=k_scales[:, half_cols(i)],
                in_=k_bf[:, 2 * i : 2 * i + 2].rearrange("p r s j -> p (r s j)"),
            )

        def cast_first(a, e, copy):
            raw = q_piece[e][:] if a == 1 else q_half[0, 0][:, :, cols(e)]
            copy(
                out=q_bf[a, 0][:, e].rearrange("p (c i) j -> p c j i", i=4),
                in_=raw.rearrange("p j (c i) -> p c j i", i=4),
            )

        def cast_dealt(a, e):
            nc.scalar.copy(
                out=q_bf[a, 1][:, e].rearrange("p (c i) j -> p c j i", i=2),
                in_=q_half[a, 1][:, :, e::2].rearrange("p j (c i) -> p c j i", i=2),
            )

        def cast_dealt_both(a):
            nc.scalar.copy(
                out=q_bf[a, 1][:].rearrange("p e (c i) j -> p c j i e", i=2),
                in_=q_half[a, 1][:].rearrange("p j (c i e) -> p c j i e", i=2, e=2),
            )

        def quant_q(a, u, e0, e1):
            part = slice(e0 * QC, e1 * QC)
            nc.vector.quantize_mx(
                out=q_codes[a, u][:, part].bitcast(FP8X4),
                scales=q_scales[a, u][:, part],
                in_=q_bf[a, u][:, e0:e1].rearrange("p e q j -> p (e q j)"),
            )

        def mask_rows(u, e):
            return m_raw[0][:, :, cols(e)] if u == 0 else m_raw[1][:, :, e::2]

        def mask_times_t(engine, u, e, part):
            engine.tensor_tensor(
                out=mt[u, e][:, part].rearrange("p (c i) r -> p c r i", i=2),
                in0=mask_rows(u, e)[:, :, part].rearrange("p r (c i) -> p c r i", i=2),
                in1=t_sb[:, 0:PACK].unsqueeze(1).unsqueeze(3).to_broadcast([P, (part.stop - part.start) // 2, PACK, 2]),
                op=ALU.mult,
            )

        def scale_mask(u, e):
            for r in range(PACK):
                nc.scalar.activation(
                    out=m_scaled[u][:, r], in_=mask_rows(u, e)[:, r], func=ACT.Copy, scale=t_sb[:, r : r + 1]
                )

        def weave_mask(u, e, part=slice(0, QC)):
            nc.scalar.copy(
                out=mt[u, e][:, part].rearrange("p (c i) r -> p c r i", i=2),
                in_=m_scaled[u][:, :, part].rearrange("p r (c i) -> p c r i", i=2),
            )

        turn = [0, 0]
        held = {}

        def scores(a, u, e, tiles):
            for g in tiles:
                held[a, u, e, g] = score_banks[g][turn[g] % SCORE_BANKS[g]]
                turn[g] = turn[g] + 1
            for r in range(PACK):
                for g in tiles:
                    rows = slice(ROWS * g, ROWS * (g + 1))
                    nc.tensor.matmul_mx(
                        out=held[a, u, e, g][:, r, :],
                        lhsT=k_codes[rows, cols(r)].bitcast(FP8X4),
                        lhsT_scale=k_scales[rows, cols(r)],
                        rhs=q_codes[a, u][rows, cols(e)].bitcast(FP8X4),
                        rhs_scale=q_scales[a, u][rows, cols(e)],
                        start=True,
                        stop=True,
                    )

        def weigh(a, u, e, g, part=slice(0, QC)):
            nc.vector.scalar_tensor_tensor(
                out=stage[a, u, e, g][:, part],
                in0=held[a, u, e, g][:, :, part].rearrange("p r q -> p q r"),
                scalar=0.0,
                in1=mt[u, e][:, part],
                op0=ALU.max,
                op1=ALU.mult,
            )

        def empty_bank(i, a, u, e, g, part=slice(0, QC)):
            src = held[a, u, e, g][:, :, part].rearrange("p r q -> p q r")
            nc.scalar.activation(out=relu_sb[i][:, part], in_=src, func=ACT.Relu)

        def weigh_pool(i, a, u, e, g, part=slice(0, QC)):
            nc.gpsimd.tensor_tensor(
                out=stage[a, u, e, g][:, part], in0=relu_sb[i][:, part], in1=mt[u, e][:, part], op=ALU.mult
            )

        def quant_w(a, u, s0, s1, src=None):
            part = slice(s0 * QC, s1 * QC)
            src = w_bf[a, u][:, s0:s1] if src is None else src
            nc.vector.quantize_mx(
                out=w_codes[a, u][:, part].bitcast(FP8X4),
                scales=w_scales[a, u][:, part],
                in_=src.rearrange("p s q r -> p (s q r)"),
            )

        def value_pass(a, u, e, g, y):
            s = slot(u, e, g)
            nc.tensor.matmul_mx(
                out=y,
                lhsT=w_codes[a, u][:, cols(s)].bitcast(FP8X4),
                lhsT_scale=w_scales[a, u][:, cols(s)],
                rhs=v_codes[:, cols(g)].bitcast(FP8X4),
                rhs_scale=v_scales[:, cols(g)],
                start=True,
                stop=True,
            )

        def values_chunk(e, b):
            for a in range(2):
                for g in range(2):
                    value_pass(a, 0, e, g, y_banks[b][:, cols(HEADS[a][g])])

        def values(a, s0, s1, b):
            for s in range(s0, s1):
                value_pass(a, 1, s % 2, s // 2, y_banks[b][:, cols(s)])

        def warm_tensor():
            for r in range(PACK):
                nc.tensor.matmul_mx(
                    out=y_banks[2][:, cols(r)],
                    lhsT=k_codes[:, cols(r)].bitcast(FP8X4),
                    lhsT_scale=k_scales[:, cols(r)],
                    rhs=q_codes[0, 0][:, cols(0)].bitcast(FP8X4),
                    rhs_scale=q_scales[0, 0][:, cols(0)],
                    start=True,
                    stop=True,
                )

        def sigmoid(i, heads):
            nc.scalar.activation(out=gate[i][:, heads], in_=og_raw[i][:, heads], func=ACT.Sigmoid)

        def gated(dst, y, g):
            nc.vector.scalar_tensor_tensor(out=dst, in0=y, scalar=1.0 / 16.0, in1=g, op0=ALU.mult, op1=ALU.mult)

        def finish_chunk(e, b):
            gated(res[e][:], y_banks[b][:].rearrange("p (h f) -> p h f", h=H), gate[e][:])
            nc.sync.dma_start(out=rows_of(out, e), in_=res[e][:])

        def finish_pair(a, b):
            gated(res[2][:, PAIR[a]], y_banks[b][:].rearrange("p (g f) -> p g f", g=2), gate[2][:, PAIR[a]])
            nc.sync.dma_start(out=rows_of(out, 2)[:, PAIR[a]], in_=res[2][:, PAIR[a]])

        def finish_head(a, g, b):
            h = HEADS[a][g]
            gated(res[2][:, h], y_banks[b][:, 2 * g * E : 2 * (g + 1) * E], gate[2][:, h])
            nc.sync.dma_start(out=rows_of(out, 2)[:, h], in_=res[2][:, h])

        def cast_v():
            nc.scalar.copy(
                out=v_bf[:].rearrange("p g (c i) j -> p g c j i", i=4),
                in_=v_raw[:].rearrange("p g j (c i) -> p g c j i", i=4),
            )

        def quant_v():
            nc.vector.quantize_mx(
                out=v_codes[:].bitcast(FP8X4), scales=v_scales[:], in_=v_bf[:].rearrange("p g e j -> p (g e j)")
            )

        every = slice(0, H)
        low, high, whole = slice(0, QC // 2), slice(QC // 2, QC), slice(0, QC)
        mid, mid_rest = slice(0, MID_SHARE), slice(MID_SHARE, QC)
        last, last_rest = slice(0, LAST_SHARE), slice(LAST_SHARE, QC)
        nc.sync.dma_start(out=k_raw[:], in_=kT.rearrange("g (p j) n -> (g p) j n", j=PACK))
        nc.scalar.dma_start(out=t_sb[:], in_=t.rearrange("(s r) o -> s (r o)", r=PACK))
        load_q_inner(0)
        load_mask(0)
        load_q_outer(q_piece[0], cols(0), slice(0, 2))
        load_q_outer(q_piece[0], cols(0), slice(2, 4))
        load_q_outer(q_piece[1], cols(1), slice(0, 2))
        load_q_outer(q_piece[1], cols(1), slice(2, 4))
        nc.vector.memset(warm[:, 0:1], 0.0)
        nc.scalar.activation(out=warm[:, 1:2], in_=warm[:, 0:1], func=ACT.Sigmoid)
        nc.gpsimd.memset(pool_in[:], 1.0)
        nc.gpsimd.tensor_tensor(out=pool_f32[:], in0=pool_in[:], in1=pool_in[:], op=ALU.mult)
        nc.gpsimd.tensor_tensor(out=pool_bf[:], in0=pool_in[:], in1=pool_in[:], op=ALU.mult)
        load_q_inner(1)
        load_mask(1)
        load_q_outer(q_half[1, 1], half_cols(1), slice(0, 1))
        load_q_outer(q_half[1, 1], half_cols(1), slice(1, 2))
        load_q_outer(q_half[1, 1], half_cols(1), slice(2, 3))
        load_q_outer(q_half[1, 1], half_cols(1), slice(3, 4))
        load_v()
        load_og(0, every)
        load_og(1, every)
        load_og(2, every)
        cast_keys()
        cast_first(0, 0, nc.vector.tensor_copy)
        cast_first(0, 1, nc.scalar.copy)
        quant_k(0)
        quant_q(0, 0, 0, 1)
        quant_k(1)
        scores(0, 0, 0, (0, 1))
        quant_q(0, 0, 1, 2)
        scores(0, 0, 1, (0, 1))

        warm_tensor()
        scale_mask(0, 1)
        cast_first(1, 0, nc.scalar.copy)
        weave_mask(0, 1)
        cast_first(1, 1, nc.scalar.copy)
        mask_times_t(nc.vector, 0, 0, low)
        mask_times_t(nc.vector, 0, 0, high)
        weigh(0, 0, 0, 0, low)
        weigh(0, 0, 0, 0, high)
        weigh(0, 0, 0, 1)
        empty_bank(0, 0, 0, 1, 1)
        cast_dealt_both(0)
        scale_mask(1, 0)
        weave_mask(1, 0)
        quant_q(1, 0, 0, 1)
        scores(1, 0, 0, (0, 1))
        quant_w(0, 0, 0, 2)
        weigh(0, 0, 1, 0)
        quant_q(1, 0, 1, 2)
        scores(1, 0, 1, (0, 1))
        weigh_pool(0, 0, 0, 1, 1)
        weigh(1, 0, 0, 0)
        weigh(1, 0, 0, 1)
        weigh(1, 0, 1, 1)
        quant_q(0, 1, 0, 2)
        scores(0, 1, 0, (0, 1))
        quant_w(0, 0, 2, 4, shared[:, 1:3])
        mask_times_t(nc.gpsimd, 1, 1, whole)
        quant_w(1, 0, 0, 2)
        weigh(1, 0, 1, 0)
        scores(0, 1, 1, (0, 1))
        empty_bank(3, 0, 1, 0, 1, mid)
        weigh_pool(3, 0, 1, 0, 1, mid)
        cast_dealt(1, 0)
        cast_dealt(1, 1)
        cast_v()
        weigh(0, 1, 0, 0)
        weigh(0, 1, 0, 1, mid_rest)
        weigh(0, 1, 1, 1)
        quant_q(1, 1, 0, 1)
        scores(1, 1, 0, (0, 1))
        quant_w(1, 0, 2, 4)
        quant_q(1, 1, 1, 2)
        scores(1, 1, 1, (0, 1))

        empty_bank(1, 1, 1, 0, 1)
        sigmoid(0, every)
        sigmoid(1, every)
        weigh(0, 1, 1, 0)
        empty_bank(2, 1, 1, 1, 1, last)
        sigmoid(2, every)
        quant_w(0, 1, 2, 4)
        quant_v()
        values_chunk(0, 0)
        values_chunk(1, 1)
        quant_w(0, 1, 0, 2)
        values(0, 0, 4, 2)
        weigh_pool(1, 1, 1, 0, 1)
        weigh_pool(2, 1, 1, 1, 1, last)
        weigh(1, 1, 0, 0)
        weigh(1, 1, 1, 0)
        finish_chunk(0, 0)
        weigh(1, 1, 1, 1, last_rest)
        finish_chunk(1, 1)
        quant_w(1, 1, 0, 2)
        values(1, 0, 2, 0)
        quant_w(1, 1, 2, 4, v_bf[:])
        values(1, 2, 4, 1)
        finish_head(0, 0, 2)
        finish_head(0, 1, 2)
        finish_head(1, 0, 0)
        finish_head(1, 1, 1)
